import numpy as np, ml_dtypes
CORES = [5,29,101,125,133,157,229,253]
N = 8
BF = ml_dtypes.bfloat16
V, K, LA, LF, Q, RO, AS, FS = 2048, 768, 256, 192, 3, 3, 170, 255
def lanes(flag, start, cap):
    order = (np.arange(K) + start) % K; fl = flag[:, order]
    o = np.argsort(~fl, axis=1, kind="stable")[:, :cap]
    return order[o], np.take_along_axis(fl, o, 1)
def judge(X, C, ids, T):
    n = ids.shape[1]; lit = np.take_along_axis(C, ids[:, None, :], 2); v = np.where(lit >= V, lit - V, lit)
    s = np.take_along_axis(X, v.reshape(8, 1, 16 * n), 2).reshape(8, 16, 16, n)
    s = np.where((lit >= V)[:, None], 63 - s, s)
    return lit, v, s, np.max(s, axis=2) < T
def states(rng, pa, pd):
    a = rng.choice(np.array(pa), (N, 8, 1)); b = rng.choice(np.array(pd), (N, 8, 1)); u = rng.random((N, 8, K))
    return np.where(u < a, 0, np.where(u >= 1 - b, 4, rng.integers(1, 4, (N, 8, K))))
def parts(rng):
    u = rng.random((N, 8, 16, K)); v = np.minimum((V * u * np.sqrt(u)).astype(np.int64), V - 1)
    T = rng.integers(58, 60, (N, 8, 1, 1)) + rng.integers(0, 2, (N, 8, 16, 1))
    return rng.integers(0, 64, (N, 8, 16, V)), v + V * rng.integers(0, 2, v.shape), states(rng, [0.3, 0.4, 0.5], [0.01, 0.05, 0.2]), T
def at(a, v):
    return np.take_along_axis(a, v.reshape(N, 8, -1), 2).reshape(v.shape)
def first(X, C, F, T):
    ia, ok = lanes(F == 0, 0, LA)
    return ia, ok & (np.sum(judge(X, C, ia, T)[3], axis=1) > Q)
def laid(rng, own, place, rest):
    X = np.zeros((8, 16, V), np.int64); C = np.zeros((8, 16, K), np.int64)
    for g in range(8):
        o = rng.permutation(V); sign = rng.integers(0, 2, V)
        s = rng.integers(0, rest[g] + 1, (16, V)); s[:, o[:K]] = own[g]
        X[g] = np.where(sign == 1, 63 - s, s)
        v = o[rng.integers(K, V, (16, K))]; v[place[g], np.arange(K)] = o[:K]
        C[g] = v + V * sign[v]
    return X, C
def full(rng):
    T = rng.integers(50, 61, (8, 16, 1)); own = rng.integers(10, 18, (8, 16, K)); place = rng.integers(0, 16, (8, K)); F = np.zeros((8, K), np.int64)
    own[[2, 7]] = 0; place[[2, 7]] = 0
    for g in range(8):
        o = rng.permutation(K); n = int(rng.integers(16, LF + 1))
        F[g, o[:n]] = rng.integers(1, 4, n); F[g, o[:16]] = 1
        own[g][:, o[:16]] = T[g] + rng.integers(0, 3, (16, 16))
    X, C = laid(rng, own, place, [9, 9, 0, 9, 9, 9, 9, 0])
    return X, C, F, T
def calm(rng):
    T = rng.integers(20, 51, (8, 16, 1)); own = np.repeat(T, K, axis=2); place = rng.integers(0, 16, (8, K)); F = rng.integers(1, 3, (8, K)); e = int(rng.integers(1, 4))
    for g in range(8):
        o = rng.permutation(K); n = 4 * int(rng.integers(2, LA >> 4)) + (e if g == 0 else 0); m = n + int(rng.integers(0, LA - n + 1)); h = m + ((K - m) >> 1)
        F[g, o[:m]] = 0
        own[g][:, o[n:h]] = 63; own[g][:, o[:n]] = T[g] - rng.integers(1, 6, (16, n))
    X, C = laid(rng, own, place, [9] * 8)
    return X, C, F, T
def pack(X, C, F, T):
    return {"xv": np.ascontiguousarray(X).reshape(N, 128, V).astype(np.float32).astype(BF), "cl": np.ascontiguousarray(C).reshape(N, 128, K).astype(np.int32),
            "fr": np.ascontiguousarray(F).astype(np.int32), "th": np.ascontiguousarray(T).reshape(N, 128, 1).astype(np.int32)}
def setup_inputs(rng):
    X, C, F, T = parts(rng)
    return pack(X, C, F, T)
def setup_inputs_spread(rng):
    low = np.minimum(np.exp2(6 * rng.random((N, 8, 1, V))) * rng.random((N, 8, 16, V)), 63).astype(np.int64)
    flip = rng.random((N, 8, V)) < 0.5; X = np.where(flip[:, :, None], 63 - low, low)
    u = rng.random((N, 8, 16, K)); v = np.minimum((V * u * u).astype(np.int64), V - 1)
    up = rng.random(v.shape) < rng.choice(np.array([0.0, 0.02, 0.06, 0.12]), (N, 8, 1, K))
    T = np.clip(61 - np.exp2(5.907 * rng.random((N, 8, 16, 1))).astype(np.int64), 1, 60)
    return pack(X, v + V * (at(flip, v) ^ up).astype(np.int64), states(rng, [0.1, 0.3, 0.6, 0.9], [0.0, 0.02, 0.3]), T)
def setup_inputs_ends(rng):
    X = 63 * rng.integers(0, 2, (N, 8, 16, V)); k = np.arange(16)[:, None]
    T = np.where(rng.random((N, 8, 16, 1)) < 0.75, 60, 1); T[:, [3, 7]] = 60; T[:, 0, 0] = 1
    u = rng.random((N, 8, K)); F = np.where(u < 0.45, 0, np.where(u < 0.75, 4, rng.choice(np.array([1, 3]), (N, 8, K))))
    m = rng.choice(np.array([16, 16, Q + 1, Q]), (N, 8, 1)); m[:, 1] = Q + 1; m[:, 2] = Q; m[:, [3, 7]] = 16
    low = np.argsort(np.argsort(rng.random((N, 8, 16)), axis=2), axis=2) < m
    X[..., 0] = np.where(low, 0, 63); X[..., V - 1] = np.where(low, 63, 0); X[..., 65] = 63
    sp = np.concatenate([np.arange(1, 65), np.arange(V - 65, V - 1)]); j = np.arange(128); cls = (j >> 1) % 3
    s = np.where(cls == 0, 59, np.where((cls == 2) & (k > Q), 63, 62)) - ((j // 6) % 2) * (k == j % 16)
    X[..., sp] = np.where(j % 2 == 1, 63 - s, s); lit = sp + V * (j % 2)
    C = np.where(rng.random((N, 8, 16, K)) < rng.choice(np.array([0.0, 0.5, 0.5, 1.0]), (N, 8, 1, K)), 0, 2 * V - 1)
    kind = rng.choice(np.array([0, 0, 0, 0, 0, 0, 0, 1, 2, 3]), (N, 8, K)); frm = rng.integers(0, 16, (N, 8, K))
    for q in range(N):
        F[q, 7] = 4; kind[q, 7] = rng.choice(np.array([0, 0, 1]), K)
        b = np.append(np.sort(AS + rng.permutation(K - 1 - AS)[:LA - 1]), K - 1)
        F[q, 7, rng.permutation(AS)[:32]] = 0; F[q, 7, b] = 0
        kind[q, 7, b[-32:]] = 2; kind[q, 7, b[-2:]] = 3; frm[q, 7, b[-2:]] = 0
    for c in range(3):
        a = lit[cls == c]; fill = a[rng.integers(0, len(a), C.shape)]
        C = np.where((kind == c + 1)[:, :, None] & (k >= frm[:, :, None]), fill, C)
    for q in range(N):
        ia, bad = first(X[q], C[q], F[q], T[q]); b = np.flatnonzero(bad[3])[:(int(np.sum(bad)) - 3) % 4]
        C[q, 3, 8, ia[3, b]] = 65
    return pack(X, C, F, T)
def setup_inputs_corners(rng):
    X, C, F, T = parts(rng); w = rng.random((N, 8, 1, K)); e = np.array([0, V - 1, V, 2 * V - 1])
    C = np.where(w < 0.15, rng.choice(e, (N, 8, 1, K)), np.where(w < 0.3, np.arange(K) + V * rng.integers(0, 2, (N, 8, 1, K)), np.where(w < 0.45, rng.choice(e, (N, 8, 16, K)), C)))
    T[:, 1] = np.where(rng.random((N, 16, 1)) < 0.3, 1, 60); T[:, 5] = 1; T[:, 6] = 60
    cases = ((0, K), (K, 0), (LA, LF), (LA + 1, LF + 1), (LA - 1, LF - 1), (1, 0), (2, K - 2), (0, 0))
    for q in range(N):
        for g in range(8):
            na, nz = cases[(g + q) % 8]; o = rng.permutation(K)
            F[q, g] = 4; F[q, g, o[:na]] = 0; F[q, g, o[na:na + nz]] = rng.integers(1, 4, nz)
    for q in range(0, N - 1, 2):
        bad = first(X[q], C[q], F[q], T[q])[1]; n = np.sum(bad[:, 0::2] & bad[:, 1::2], axis=1); c = 0
        for g in range(8):
            if n[g] < 2: continue
            d = int(n[g]) + (0, 1, -1)[c % 3]; c += 1
            z = rng.integers(0, 4, K); z[rng.permutation(K)[:d]] = 4; F[q + 1, g] = z
    return pack(X, C, F, T)
def setup_inputs_ties(rng):
    b = rng.choice(np.array([9, 30, 60]), (N, 8, 1, 1)); T = np.zeros((N, 8, 16, 1), np.int64) + b; i = np.arange(16)[:, None]
    mul = 2 * rng.integers(0, 8, (N, 8, 1, V)) + 1; sh = rng.integers(0, 16, (N, 8, 1, V)); n = Q + rng.integers(0, 2, (N, 8, 1, V))
    odd = np.arange(V) % 2 == 1
    s = np.where(odd & ((i * mul + sh) % 16 >= n), b + rng.integers(0, 4, (N, 8, 1, V)), b - 1 - rng.integers(0, 2, (N, 8, 1, V)))
    flip = rng.random((N, 8, V)) < 0.5; X = np.where(flip[:, :, None], 63 - s, s)
    lim = rng.choice(np.array([V // 2, V // 2, V // 16]), (N, 8, 1, 1))
    v = 2 * np.minimum((rng.random((N, 8, 16, K)) * lim).astype(np.int64), lim - 1)
    one = (i == rng.integers(0, 16, (N, 8, 1, K))) & (rng.random((N, 8, 1, K)) < 0.9)
    v = np.where(one, 2 * rng.integers(0, V // 2, v.shape) + 1, v)
    return pack(X, v + V * at(flip, v).astype(np.int64), states(rng, [0.3, 0.4, 0.5], [0.02, 0.1, 0.2]), T)
def setup_inputs_alike(rng):
    X, C, F, T = parts(rng); few = rng.integers(0, V, (N, 8, 24)); few[:, :, 0] = 0; few[:, :, 1] = V - 1
    v = np.take_along_axis(few, rng.integers(0, 24, (N, 8, 16 * K)), 2).reshape(N, 8, 16, K) + V * rng.integers(0, 2, (N, 8, 16, K))
    C[:, ::2] = v[:, ::2]
    for q in range(N): C[q, 5] = C[q, 5][:, rng.integers(0, 8, K)]
    o = rng.permutation(N)
    X[o[0]], C[o[0]], F[o[0]], T[o[0]] = full(rng)
    X[o[1]], C[o[1]], F[o[1]], T[o[1]] = calm(rng)
    return pack(X, C, F, T)
def check_inputs(d):
    bad = []
    for k, lo, hi in (("xv", 0, 63), ("cl", 0, 2 * V - 1), ("fr", 0, 4), ("th", 1, 60)):
        a = np.asarray(d[k]).astype(np.float64)
        if not np.all((a >= lo) & (a <= hi)): bad.append("range of " + k)
        elif not np.all(a == np.floor(a)): bad.append("whole numbers of " + k)
    return bad
def reference(xv, cl, fr, th):
    X = xv.astype(np.float32).astype(np.int64).reshape(N, 8, 16, V); C = cl.astype(np.int64).reshape(N, 8, 16, K); F = fr.astype(np.int64).reshape(N, 8, K)
    TH = th.astype(np.int64).reshape(N, 8, 16, 1); A = np.zeros(N, np.int64)
    for t in range(RO):
        nX = np.array(X); nC = np.array(C); nF = np.array(F); sent = []
        for r in range(N):
            T = TH[r] + (A[r] & 3)
            ia, oka = lanes(F[r] == 0, AS * t % K, LA); iz, okz = lanes((F[r] >= 1) & (F[r] <= 3), FS * t % K, LF)
            lit, v, s, fail = judge(X[r], C[r], ia, T); bad = oka & (np.sum(fail, axis=1) > Q); A[r] = np.sum(bad)
            m = oka & ~bad; nF[r][np.nonzero(m)[0], ia[m]] = 1
            wake = np.sum(judge(X[r], C[r], iz, T)[3], axis=1) > Q
            old = np.take_along_axis(F[r], iz, 1); nF[r][np.nonzero(okz)[0], iz[okz]] = np.where(wake, 0, old + 1)[okz]
            kk = np.argmax(np.sum(s * fail[:, :, None, :], axis=1), axis=1)[:, None, :]
            pick = np.take_along_axis(lit, kk, 1); pv = np.take_along_axis(v, kk, 1)[:, 0]
            up = np.minimum(np.take_along_axis(s, kk[:, None], 2)[:, :, 0] + 8, 63); new = np.where(pick >= V, 63 - up, up)
            for g in range(8):
                b = np.flatnonzero(bad[g]); u, ix = np.unique(pv[g, b], return_index=True); w = b[ix]
                nX[r, g][:, u] = np.where(fail[g][:, w], new[g][:, w], X[r, g][:, u])
            tot = np.sum(s, axis=1)
            sent.append((bad[:, 0::2] & bad[:, 1::2], np.where(tot[:, :, 1::2] > tot[:, :, 0::2], lit[:, :, 1::2], lit[:, :, 0::2])))
        for r in range(N):
            a = (r + 1 + t % 3) % N; both, joint = sent[r]
            for g in range(8):
                come = joint[g][:, both[g]]; dead = np.flatnonzero(F[a, g] == 4); n = min(come.shape[1], len(dead))
                nC[a, g][:, dead[:n]] = come[:, :n]; nF[a, g][dead[:n]] = 0
        X = nX; C = nC; F = nF
    return {"yx": X.reshape(N, 128, V).astype(np.float32).astype(BF), "yc": C.reshape(N, 128, K).astype(np.float32), "yf": F.astype(np.float32)}

@@ -1,0 +1,512 @@
+import numpy as np
+from concourse.mybir import dt, AluOpType, AxisListType, ActivationFunctionType
+
+A_, F_ = AluOpType, ActivationFunctionType
+N, V, K, LA, LF, RO, AS, FS = 8, 2048, 768, 256, 192, 3, 170, 255
+BRK = sorted(set([0] + [AS * t % K for t in range(RO)] + [FS * t % K for t in range(RO)])) + [K]
+SEG = []
+_p = 0
+for _a, _b in zip(BRK[:-1], BRK[1:]):
+    SEG.append((_a, _p, _b - _a))
+    _p += -(-(_b - _a) // 16) * 16
+NP = _p
+Q = NP // 16
+START = {a: p // 16 for a, p, n in SEG}
+XB = 256
+SB = XB + 2 * V
+WW = SB + 16
+FB0 = K
+LW = 2 * K + NP
+JW = 132
+CW = NP + JW
+JT = 136 + 128
+CH = 64
+NA, NF = LA // CH, LF // CH
+
+SCRATCH = {
+    "W": ("sbuf", [128, WW], "bfloat16"), "S": ("sbuf", [128, 16 * LA], "bfloat16"), "M": ("sbuf", [128, 16 * LA], "bfloat16"),
+    "Z": ("sbuf", [128, 16 * LA], "bfloat16"), "S2": ("sbuf", [128, 16 * LF], "bfloat16"), "M2": ("sbuf", [128, 16 * LF], "bfloat16"),
+    "C0": ("sbuf", [128, CW], "float32"), "C1": ("sbuf", [128, CW], "float32"), "C2": ("sbuf", [128, CW], "float32"),
+    "C3": ("sbuf", [128, CW], "float32"), "CI": ("sbuf", [128, K], "int32"), "LN": ("sbuf", [128, LW], "float32"),
+    "YW": ("sbuf", [128, LW], "bfloat16"), "OA": ("sbuf", [128, LA], "uint16"), "OF": ("sbuf", [128, LF], "uint16"),
+    "FR": ("sbuf", [8, K], "int32"), "FRB": ("sbuf", [8, NP], "bfloat16"), "TI": ("sbuf", [128, 1], "int32"),
+    "TH": ("sbuf", [128, 1], "float32"), "TT": ("sbuf", [128, 1], "float32"), "AI": ("sbuf", [128, 2], "int32"),
+    "ONE": ("sbuf", [128, NP], "bfloat16"), "PM": ("sbuf", [16, NP], "bfloat16"), "QM": ("sbuf", [8, 128], "bfloat16"),
+    "QM0": ("sbuf", [8, 128], "bfloat16"), "LT": ("sbuf", [16, 256], "bfloat16"), "ID": ("sbuf", [128, 128], "bfloat16"),
+    "DM": ("sbuf", [128, NP], "bfloat16"), "TRI": ("sbuf", [128, 256], "bfloat16"), "BO": ("sbuf", [128, 128], "bfloat16"),
+    "BOF": ("sbuf", [128, 128], "float32"), "TS": ("sbuf", [128, 128], "bfloat16"), "SH": ("sbuf", [128, 128], "float32"),
+    "DF": ("sbuf", [128, 128], "float32"), "D1024": ("sbuf", [128, 128], "bfloat16"), "D8": ("sbuf", [128, 128], "bfloat16"),
+    "I4": ("sbuf", [128, 128], "bfloat16"), "NI4": ("sbuf", [128, 128], "bfloat16"), "I16": ("sbuf", [128, 8], "bfloat16"),
+    "NIN": ("sbuf", [128, 8], "bfloat16"), "O32": ("sbuf", [128, 128], "float32"), "KV": ("sbuf", [128, 1], "float32"),
+    "KC0": ("sbuf", [1, 256], "bfloat16"), "KC1": ("sbuf", [1, 256], "bfloat16"), "KW": ("sbuf", [128, 128], "bfloat16"),
+    "WC": ("sbuf", [128, 128], "bfloat16"), "L15": ("sbuf", [128, 16], "uint16"),
+    "LQI": ("sbuf", [128, 68], "int32"), "LQ": ("sbuf", [128, 52], "uint16"), "CL0": ("sbuf", [2, 128], "bfloat16"),
+    "CL": ("sbuf", [2, 128], "bfloat16"), "CR0": ("sbuf", [2, 2 * Q], "bfloat16"), "CR": ("sbuf", [2, 2 * Q], "bfloat16"),
+    "PD": ("sbuf", [128, Q], "float32"), "J0": ("sbuf", [128, Q], "float32"), "JD": ("sbuf", [128, 8], "float32"),
+    "U0": ("sbuf", [2 * Q, 2 * Q], "bfloat16"), "U1": ("sbuf", [2 * Q, 2 * Q], "bfloat16"), "U2": ("sbuf", [2 * Q, 2 * Q], "bfloat16"),
+    "UT": ("sbuf", [2 * Q, 2 * Q], "bfloat16"), "SEGM": ("sbuf", [128, 1024], "bfloat16"), "RST": ("sbuf", [128, 1024], "bfloat16"),
+    "DC": ("sbuf", [128, Q], "float32"), "T2": ("sbuf", [128, Q], "float32"), "T1": ("sbuf", [128, Q], "float32"),
+    "FW": ("sbuf", [128, NP], "bfloat16"), "FWS": ("sbuf", [128, NP], "bfloat16"), "FL": ("sbuf", [128, 3 * Q], "bfloat16"),
+    "GE": ("sbuf", [128, Q], "bfloat16"), "O1": ("sbuf", [2 * Q, 128], "bfloat16"), "O2": ("sbuf", [Q, 128], "bfloat16"),
+    "MM": ("sbuf", [128, 2 * Q], "float32"), "PS": ("sbuf", [128, 2 * Q], "float32"), "PL": ("sbuf", [128, 52], "uint16"),
+    "F1": ("sbuf", [128, Q], "float32"), "DD": ("sbuf", [128, Q], "float32"), "E0": ("sbuf", [128, Q], "float32"),
+    "E1": ("sbuf", [128, Q], "float32"), "NT": ("sbuf", [128, Q], "float32"), "IXF": ("sbuf", [128, 2 * Q], "float32"),
+    "IX": ("sbuf", [128, 52], "uint16"), "FA": ("sbuf", [128, LA], "bfloat16"), "FA2": ("sbuf", [128, LF], "bfloat16"),
+    "VV": ("sbuf", [128, LA], "bfloat16"), "SG": ("sbuf", [128, LA], "bfloat16"), "DLV": ("sbuf", [128, LA], "float32"),
+    "DLS": ("sbuf", [128, LA], "bfloat16"), "DEO": ("sbuf", [128, 128], "float32"), "VI": ("sbuf", [128, LA], "bfloat16"),
+    "BT": ("sbuf", [128, 128], "bfloat16"), "INC": ("sbuf", [128, 128], "float32"), "IB": ("sbuf", [128, 128], "float32"),
+    "IBD": ("sbuf", [128, 128], "float32"), "IS": ("sbuf", [128, 128], "float32"), "JL": ("sbuf", [128, 8], "float32"),
+    "JLU": ("sbuf", [128, 8], "uint16"), "R": ("sbuf", [128, 256], "float32"), "EQ": ("sbuf", [128, 256], "bfloat16"),
+    "HV": ("sbuf", [128, 256], "float32"), "HS": ("sbuf", [128, 256], "bfloat16"), "VM": ("sbuf", [128, 256], "float32"),
+    "CS": ("sbuf", [128, 256], "float32"), "GL": ("sbuf", [128, 16], "uint16"), "VT": ("sbuf", [128, 256], "float32"),
+    "EE": ("sbuf", [128, 256], "bfloat16"), "ES": ("sbuf", [128, 256], "bfloat16"), "W1": ("sbuf", [128, 48], "float32"),
+    "SL": ("sbuf", [128, 32], "uint16"), "FSG": ("sbuf", [128, 256], "float32"), "XN": ("sbuf", [128, 256], "bfloat16"),
+    "XC": ("sbuf", [128, 256], "bfloat16"), "GT": ("sbuf", [128, 128], "bfloat16"), "PJ": ("sbuf", [128, 128], "float32"),
+    "JB": ("sbuf", [128, JT], "float32"), "SGA": ("sbuf", [128, 1], "float32"), "SGJ": ("sbuf", [128, LA], "float32"),
+    "YF8": ("sbuf", [8, K], "float32"), "FBB": ("sbuf", [128, 64], "bfloat16"),
+    "RL0": ("sbuf", [128, JW], "float32"), "RL2": ("sbuf", [128, JW], "float32"),
+}
+for _i in range(8):
+    SCRATCH["B%d" % _i] = ("psum", [128, 512], "float32")
+SEMAPHORES = ["sV", "sS", "sP", "sG"] + ["ld%d" % i for i in range(6)] + ["st%d" % i for i in range(14)] \
+    + ["arr%d" % i for i in range(RO)] + ["ls%d" % i for i in range(RO)] + ["ra%d" % i for i in range(RO)]
+
+
+def route(topo, src, dst):
+    if topo.may_write(src, dst):
+        return None
+    c = [r for r in topo.cores_of(src) if r != src and topo.may_write(r, dst)]
+    return sorted(c, key=lambda r: (topo.die(r) != topo.die(src), r))[0]
+
+
+def emask(topo, src, dst):
+    m = 0
+    for e in topo.engines(src, dst)[:8]:
+        m |= 1 << e
+    return m
+
+
+def relay_program(g, core, T, topo):
+    for r in range(N):
+        src = T.cores[r]
+        for t in range(RO):
+            dst = T.cores[(r + 1 + t % 3) % N]
+            if route(topo, src, dst) == core:
+                rid, pid = topo.addr(dst, core)
+                buf = T["RL%d" % t]
+                g.wait_ge(T.sem["ra%d" % t], 8)
+                g.remote_dma(T["C%d" % t][:, NP:CW], buf[:, 0:JW], T.sem["arr%d" % t], T.sem["ls%d" % t], pid, rid, emask(topo, core, dst))
+    for r in range(N):
+        for t in range(RO):
+            if route(topo, T.cores[r], T.cores[(r + 1 + t % 3) % N]) == core:
+                g.wait_ge(T.sem["ls%d" % t], 8)
+
+
+def rank_program(g, core, T, topo):
+    rank = T.rank_of(core)
+    if rank is None:
+        relay_program(g, core, T, topo)
+        return
+    eng = {"V": g.vector, "S": g.scalar, "P": g.tensor, "G": g, "Y": g.sync}
+    cnt = {"V": 0, "S": 0, "P": 0, "G": 0}
+    known = {q: {} for q in eng}
+    hist = {}
+    bits = {}
+    serial = [0]
+
+    def cols(lo, n, step):
+        k = (lo, n, step)
+        if k not in bits:
+            m = 0
+            for i in range(n):
+                m |= 1 << (lo + i * step)
+            bits[k] = m
+        return bits[k]
+
+    def a(buf, lo=0, n=None, step=1, p=None, p0=0):
+        if n is None:
+            n = T[buf].shape[1] - lo
+        p = T[buf].shape[0] if p is None else p
+        return (T[buf][p0:p0 + p, lo:lo + (n - 1) * step + 1:step] if step > 1 else T[buf][p0:p0 + p, lo:lo + n], buf, cols(lo, n, step))
+
+    def ind(w, o):
+        return (w[0].indirect(o[0]), w, o)
+
+    def acc(x):
+        return [x] if len(x) == 3 and isinstance(x[1], str) else [x[1], x[2]]
+
+    def need(q, tag, reads, writes):
+        want = {}
+        for w, lst in ((False, reads), (True, writes)):
+            for _, buf, m in lst:
+                ps = buf[0] == "B" and buf[1:].isdigit()
+                for (em, ew, eq, sem, val, snap) in hist.get(buf, []):
+                    hit = em & m
+                    if ps and eq != tag:
+                        pass
+                    elif not hit or not (w or ew):
+                        continue
+                    elif eq == tag and (not ew or (w and q == "P")):
+                        continue
+                    if known[q].get(sem, 0) >= val:
+                        continue
+                    if sem not in want or want[sem][0] < val:
+                        want[sem] = (val, snap)
+        for sem in list(want):
+            val = want[sem][0]
+            if any(o != sem and want[o][1].get(sem, 0) >= val for o in want):
+                del want[sem]
+        for sem in want:
+            val, snap = want[sem]
+            eng[q].wait_ge(T.sem[sem], val)
+            for k, x in snap.items():
+                if known[q].get(k, 0) < x:
+                    known[q][k] = x
+            known[q][sem] = max(known[q].get(sem, 0), val)
+
+    def note(tag, reads, writes, sem, val, snap):
+        for _, buf, m in writes:
+            h = hist.setdefault(buf, [])
+            h[:] = [e for e in h if e[0] & ~m] if not (buf[0] == "B" and buf[1:].isdigit()) else [e for e in h if e[2] != tag or e[0] & ~m]
+            h.append((m, True, tag, sem, val, snap))
+        for _, buf, m in reads:
+            h = hist.setdefault(buf, [])
+            h[:] = [e for e in h if e[1] or e[2] != tag or e[0] & ~m]
+            h.append((m, False, tag, sem, val, snap))
+
+    def run(q, fn, out, ins):
+        writes = acc(out)[:1] if isinstance(out, tuple) else out
+        reads = acc(out)[1:] if isinstance(out, tuple) else []
+        for x in ins:
+            reads = reads + acc(x)
+        need(q, q, reads, writes)
+        cnt[q] += 1
+        fn().then_inc(T.sem["s" + q], 1)
+        snap = dict(known[q])
+        snap["s" + q] = cnt[q]
+        note(q, reads, writes, "s" + q, cnt[q], snap)
+
+    def dma(q, out, in_, sem, reads, writes):
+        need(q, None, reads, writes)
+        eng[q].dma_start(out, in_).then_inc(T.sem[sem], 16)
+        serial[0] += 1
+        note("d%d" % serial[0], reads, writes, sem, 16, dict(known[q]))
+
+    def ap(x):
+        return x[0]
+
+    def copy(out, in_):
+        run("V", lambda: g.vector.tensor_copy(ap(out), ap(in_)), out, [in_])
+
+    def tt(out, x, y, op):
+        run("V", lambda: g.vector.tensor_tensor(ap(out), ap(x), ap(y), op), out, [x, y])
+
+    def ts(out, x, s1, op0, s2=None, op1=None):
+        ins = [x] + [s for s in (s1, s2) if isinstance(s, tuple)]
+        u1 = s1[0] if isinstance(s1, tuple) else s1
+        if op1 is None:
+            run("V", lambda: g.vector.tensor_scalar(ap(out), ap(x), u1, None, op0), out, ins)
+        else:
+            run("V", lambda: g.vector.tensor_scalar(ap(out), ap(x), u1, s2, op0, op1), out, ins)
+
+    def scan(out, d0, d1, ini, op0, op1):
+        run("V", lambda: g.vector.tensor_tensor_scan(ap(out), ap(d0), ap(d1), ini, op0, op1), out, [d0, d1])
+
+    def fill(out, c):
+        run("V", lambda: g.vector.memset(ap(out), c), out, [])
+
+    def act(out, x, func, bias=0.0, scale=1.0, accum=None):
+        ins = [x] + ([bias] if isinstance(bias, tuple) else [])
+        b = bias[0] if isinstance(bias, tuple) else bias
+        if accum is None:
+            run("S", lambda: g.scalar.activation(ap(out), ap(x), func, bias=b, scale=scale), out, ins)
+        else:
+            run("S", lambda: g.scalar.activation(ap(out), ap(x), func, bias=b, scale=scale, accum_out=ap(accum)), [out, accum], ins)
+
+    def mm(out, l, r, start, stop):
+        run("P", lambda: g.tensor.matmul(ap(out), ap(l), ap(r), start, stop), out, [l, r])
+
+    def iota(out, pat, base, cm):
+        run("G", lambda: g.iota(ap(out), pat, base, cm, allow_small_or_imprecise_dtypes=True), out, [])
+
+    def sel(out, x, pat, op, fl, base, cm):
+        run("G", lambda: g.affine_select(ap(out), ap(x), pat, op, fl, base, cm), out, [x])
+
+    dma("Y", T.FR[:], T.fr[:], "ld0", [], [a("FR")])
+    dma("S", T.TI[:], T.th[:], "ld1", [], [a("TI")])
+    dma("Y", T.CI[:], T.cl[:], "ld2", [], [a("CI")])
+    dma("S", T.W[:, XB:XB + V], T.xv[:], "ld3", [], [a("W", XB, V)])
+
+    fill(a("ONE"), 1.0)
+    fill(a("FRB"), 8.0)
+    sel(a("PM"), a("ONE", p=16), [[0, Q], [1, 16]], A_.is_equal, 0.0, 0, -1)
+    sel(a("QM0"), a("ONE", 0, 128, p=8), [[1, 128]], A_.is_ge, 0.0, 0, -16)
+    sel(a("QM"), a("QM0"), [[-1, 128]], A_.is_ge, 0.0, 15, 16)
+    fill(a("SEGM"), 1.0)
+    fill(a("SEGM", 0, 64, 16), 0.0)
+    mm(a("B1", 0, 512), a("PM", 0, 128), a("PM", 0, 512), True, True)
+    mm(a("B2", 0, NP - 512), a("PM", 0, 128), a("PM", 512, NP - 512), True, True)
+    mm(a("B3", 0, 128), a("QM"), a("QM"), True, True)
+    copy(a("DM", 0, 512), a("B1", 0, 512))
+    copy(a("DM", 512, NP - 512), a("B2", 0, NP - 512))
+    copy(a("BO"), a("B3", 0, 128))
+    for s0, p0, n in SEG:
+        copy(a("FRB", p0, n), a("FR", s0, n))
+    mm(a("B4", 0, 512), a("QM"), a("FRB", 0, 512), True, True)
+    mm(a("B5", 0, NP - 512), a("QM"), a("FRB", 512, NP - 512), True, True)
+    tt(a("FW", 0, 512), a("B4", 0, 512), a("DM", 0, 512), A_.mult)
+    tt(a("FW", 512, NP - 512), a("B5", 0, NP - 512), a("DM", 512, NP - 512), A_.mult)
+    scan(a("FWS"), a("SEGM", 0, NP), a("FW"), 0.0, A_.mult, A_.add)
+    copy(a("T2"), a("FWS", 15, Q, 16))
+    sel(a("TS"), a("BO"), [[1, 128]], A_.is_ge, 0.0, -1, -1)
+    iota(a("CL0"), [[0, 8], [1, 16]], 0, 0)
+    sel(a("CL"), a("CL0"), [[0, 128]], A_.is_gt, 1.0, 0, 1)
+    iota(a("CR0", 0, Q), [[-16, Q]], -2 * K, 0)
+    iota(a("CR0", Q, Q), [[-16, Q]], -K, 0)
+    sel(a("CR"), a("CR0"), [[0, 2 * Q]], A_.is_equal, -1.0, 0, 1)
+
+    def order(t):
+        for b, s in ((0, START[AS * t % K]), (Q, START[FS * t % K])):
+            u = "U%d" % t
+            n = Q - s
+            sel(a("UT", b + s, n, p=2 * Q), a("ONE", 0, n, p=2 * Q), [[1, n]], A_.is_gt, 0.0, b + s, -1)
+            sel(a(u, b + s, n), a("UT", b + s, n), [[0, n]], A_.is_ge, 0.0, -(b + s), 1)
+            if s:
+                sel(a(u, b, s), a("ONE", 0, s, p=2 * Q), [[0, s]], A_.is_ge, 0.0, b + Q - 1, -1)
+                sel(a("UT", b, s), a(u, b, s), [[0, s]], A_.is_ge, 0.0, -(b + s), 1)
+                sel(a(u, b, s), a("UT", b, s), [[-1, s]], A_.is_ge, 1.0, -b, 1)
+                if b:
+                    sel(a("UT", b, s), a(u, b, s), [[0, s]], A_.is_ge, 0.0, -b, 1)
+                    sel(a(u, b, s), a("UT", b, s), [[0, s]], A_.is_ge, 0.0, -b, 1)
+
+    order(0)
+    mm(a("B6", 0, Q), a("CL"), a("CR", 0, Q), True, True)
+    ts(a("PD"), a("B6", 0, Q), -1.0, A_.mult)
+    ts(a("J0"), a("PD"), -2.0 * K, A_.add)
+    ts(a("JD"), a("J0", 0, 8), 136.0 - 512.0, A_.add)
+    iota(a("LN", 0, LA), [[0, LA]], 2 * V, 0)
+    iota(a("LN", FB0, LF), [[0, LF]], 2 * V, 0)
+
+    def lists(t):
+        ts(a("FL", 0, Q), a("T2"), 0.0, A_.is_le)
+        ts(a("GE"), a("T2"), 0.0, A_.is_gt)
+        ts(a("FL", 2 * Q, Q), a("T2"), 3.5, A_.is_ge)
+        tt(a("FL", Q, Q), a("GE"), a("FL", 2 * Q, Q), A_.subtract)
+        mm(a("B7", 0, 128, p=2 * Q), a("FL", 0, 2 * Q), a("BO"), True, True)
+        act(a("O1"), a("B7", 0, 128, p=2 * Q), F_.Identity)
+        mm(a("B6", 0, 2 * Q), a("TS"), a("FL", 0, 2 * Q), True, False)
+        mm(a("B6", 0, 2 * Q), a("CL"), a("CR"), False, False)
+        mm(a("B6", 0, 2 * Q), a("O1"), a("U%d" % t), False, True)
+        ts(a("F1"), a("T2"), 0.0, A_.max, 1.0, A_.add)
+        tt(a("MM"), a("B6", 0, 2 * Q), a("FL", 0, 2 * Q), A_.mult)
+        tt(a("PS", 0, Q), a("MM", 0, Q), a("MM", Q, Q), A_.add)
+        tt(a("PS", Q, Q), a("PS", 0, Q), a("PD"), A_.add)
+        copy(a("PL", 0, Q), a("PS", Q, Q))
+        copy(ind(a("LN"), a("PL", 0, Q)), a("C%d" % t, 0, NP))
+        copy(a("OA"), a("LN", 0, LA))
+        mm(a("B5", 0, 128, p=Q), a("FL", 2 * Q, Q), a("BO"), True, True)
+        act(a("O2"), a("B5", 0, 128, p=Q), F_.Identity)
+        mm(a("B5", 128, Q), a("TS"), a("FL", 2 * Q, Q), True, False)
+        mm(a("B5", 128, Q), a("NI4"), a("FL", 2 * Q, Q), False, False)
+        mm(a("B5", 128, Q), a("O2"), a("U0", 0, Q, p=Q), False, True)
+
+    def gather(q, c, out, off):
+        w = ind(a("W", XB, WW - XB), a(off, CH * c, CH))
+        if q == "V":
+            copy(a(out, 16 * CH * c, 16 * CH), w)
+        else:
+            act(a(out, 16 * CH * c, 16 * CH), w, F_.Identity)
+
+    def negate(lo, n, q):
+        if q == "V":
+            ts(a("W", XB + V + lo, n), a("W", XB + lo, n), -1.0, A_.mult, 63.0, A_.add)
+        else:
+            act(a("W", XB + V + lo, n), a("W", XB + lo, n), F_.Identity, 63.0, -1.0)
+
+    for s0, p0, n in SEG:
+        fill(a("C0", p0 + n, -(-n // 16) * 16 - n), 0.0)
+        copy(a("C0", p0, n), a("CI", s0, n))
+    sel(a("ID"), a("ONE", 0, 128), [[-1, 128]], A_.is_equal, 0.0, 0, 1)
+    ts(a("NI4"), a("ID"), -4096.0, A_.mult)
+    lists(0)
+    negate(0, 1344, "V")
+    negate(1344, V - 1344, "S")
+    fill(a("W", SB, 16), 200.0)
+    fill(a("W", 0, XB), 0.0)
+    fill(a("RST"), 64.0)
+    fill(a("RST", 0, 64, 16), 8192.0)
+    copy(a("TH"), a("TI"))
+    copy(a("TT"), a("TI"))
+    pads = 0
+    for s0, p0, n in SEG:
+        fill(a("DC", p0 // 16, -(-n // 16)), 4096.0 - 513.0 - pads)
+        pads += -(-n // 16) * 16 - n
+    ts(a("PS", 0, Q), a("T2"), 6.0, A_.is_ge, 4096.0, A_.mult)
+    tt(a("DC"), a("DC"), a("PS", 0, Q), A_.add)
+    fill(a("YW"), 1.0)
+    fill(a("FBB"), 0.0)
+    fill(a("JB"), 0.0)
+    fill(a("O32"), 1.0 / 32)
+    copy(a("BOF"), a("BO"))
+    sel(a("SH"), a("BOF"), [[-1, 128]], A_.is_equal, 0.0, -1, 1)
+    tt(a("DF"), a("ID"), a("SH"), A_.subtract)
+    ts(a("D1024"), a("DF"), -1024.0, A_.mult)
+    ts(a("D8"), a("DF"), -8.0, A_.mult)
+    ts(a("I4"), a("ID"), 4096.0, A_.mult)
+    ts(a("I16"), a("BO", 0, 8, 16), 16.0, A_.mult)
+    ts(a("NIN"), a("BO", 0, 8, 16), -1.0, A_.mult)
+    ts(a("KV"), a("DM", 15, 1), float(XB - V // 2 - 4096), A_.mult)
+    iota(a("KC0"), [[0, 16], [-16384, 16]], 262144, 0)
+    iota(a("KC1"), [[0, 16], [-1, 16]], 15, 0)
+    iota(a("KW"), [[0, 8], [1024, 16]], -16384, 0)
+    tt(a("WC"), a("BO"), a("KW"), A_.mult)
+    iota(a("LQI", 52, 16), [[16, 16]], 15, 0)
+    copy(a("L15"), a("LQI", 52, 16))
+    iota(a("LQI", 0, 52), [[1, 52]], 0, 0)
+    copy(a("LQ"), a("LQI", 0, 52))
+    sel(a("LT"), a("ONE", 0, 256, p=16), [[0, 16], [-1, 16]], A_.is_ge, 0.0, -1, 1)
+    mm(a("B4", 0, 256), a("PM", 0, 128), a("LT"), True, True)
+    act(a("TRI"), a("B4", 0, 256), F_.Identity)
+
+    for t in range(RO):
+        dst = T.cores[(rank + 1 + t % 3) % N]
+        C = "C%d" % t
+        gather("S", 0, "S", "OA")
+        gather("V", 1, "S", "OA")
+        gather("S", 2, "S", "OA")
+        gather("S", 3, "S", "OA")
+        copy(a("OF"), a("LN", FB0, LF))
+        tt(a("DEO"), a("LN", 1, 128, 2), a("LN", 0, 128, 2), A_.subtract)
+        tt(a("DD"), a("B5", 128, Q), a("DC"), A_.add)
+        ts(a("E1"), a("DD"), 513.0 + NP, A_.add)
+        tt(a("E0"), a("J0"), a("E1"), A_.subtract)
+        act(a("SG"), a("LN", 0, LA), F_.Sign, 0.5 - V)
+        for h in range(2):
+            mm(a("B2", 128 * h, 128), a("DF"), a("LN", h, 128, 2), True, False)
+            mm(a("B2", 128 * h, 128), a("D1024"), a("SG", h, 128, 2), False, True)
+            mm(a("B2", 256 + 128 * h, 128), a("D8"), a("SG", h, 128, 2), True, True)
+        act(a("DLV"), a("B2", 0, 256), F_.Identity, a("KV"))
+        act(a("DLS"), a("B2", 256, 256), F_.Identity)
+        mm(a("B0", 0, 256), a("ONE", 0, 128, p=1), a("KC0"), True, False)
+        for c in range(NF):
+            gather("S", c, "S2", "OF")
+        for c in range(NA):
+            lo = 16 * CH * c
+            scan(a("M", lo, 16 * CH), a("SEGM"), a("S", lo, 16 * CH), 0.0, A_.mult, A_.max)
+            ts(a("FA", CH * c, CH), a("M", lo + 15, CH, 16), a("TT"), A_.is_lt)
+            ts(a("VV", CH * c, CH), a("FA", CH * c, CH), 2048.0, A_.mult, -1024.0, A_.add)
+            tt(a("S", lo, CH, 16), a("VV", CH * c, CH), a("M", lo, CH, 16), A_.min)
+            scan(a("Z", lo, 16 * CH), a("RST"), a("S", lo, 16 * CH), 0.0, A_.add, A_.min)
+            if c == NA - 1:
+                mm(a("B4", 0, LA), a("BO"), a("FA"), True, True)
+            for h in range(2):
+                mm(a("B0", 128 * h, 128, p=32, p0=32 * c), a("FA", CH * c + h, 32, 2), a("WC"), False, False)
+            for h in range(2):
+                for k in range(16):
+                    mm(a("B0", 128 * h + k, 8, 16, p=32, p0=32 * c), a("Z", lo + 16 * h + k, 32, 32), a("I16"), False, False)
+        mm(a("B0", 0, 256), a("ONE", 0, 128, p=1), a("KC1"), False, True)
+        ts(a("VI"), a("B4", 0, LA), 3.5, A_.is_gt)
+        act(a("YW", 0, LA), a("B4", 0, LA), F_.Relu, -25.0, 8.0)
+        act(a("SGJ"), a("B4", 0, LA), F_.Sign, -3.5, 1.0, a("SGA"))
+        tt(a("BT"), a("VI", 0, 128, 2), a("VI", 1, 128, 2), A_.mult)
+        scan(a("INC"), a("ONE", 0, 128), a("BT"), -513.0, A_.mult, A_.add)
+        tt(a("IB"), a("INC"), a("BT"), A_.mult)
+        tt(a("IBD"), a("IB"), a("DM", 0, 128), A_.mult)
+        scan(a("IS"), a("SEGM", 0, 128), a("IBD"), 0.0, A_.mult, A_.add)
+        tt(a("JL"), a("IS", 15, 8, 16), a("JD"), A_.min)
+        ts(a("JLU"), a("JL"), 512.0, A_.add)
+        copy(a("JB", 128, 1), a("INC", 127, 1))
+        scan(a("R"), a("SEGM", 0, 256), a("B0", 0, 256), 0.0, A_.mult, A_.max)
+        scan(a("VT"), a("SEGM", 0, 256), a("B0", 0, 256), 0.0, A_.mult, A_.max)
+        tt(a("EQ"), ind(a("R"), a("L15")), a("VT"), A_.is_equal)
+        for h in range(2):
+            mm(a("B3", 128 * h, 128), a("EQ", 128 * h, 128), a("ID"), True, True)
+        scan(a("M2", 0, 1024), a("SEGM"), a("S2", 0, 1024), 0.0, A_.mult, A_.max)
+        tt(a("HV"), a("B3", 0, 256), a("DLV"), A_.mult)
+        tt(a("HS"), a("B3", 0, 256), a("DLS"), A_.mult)
+        for h in range(2):
+            mm(a("B1", h, 128, 2), a("BOF"), a("HV", 128 * h, 128), True, False)
+            mm(a("B1", h, 128, 2), a("I4"), a("VI", h, 128, 2), False, True)
+        for h in range(2):
+            mm(a("B7", h, 128, 2), a("BO"), a("HS", 128 * h, 128), True, True)
+        scan(a("M2", 1024, 1024), a("SEGM"), a("S2", 1024, 1024), 0.0, A_.mult, A_.max)
+        for k in range(16):
+            mm(a("B2", k, 8, 16), a("S", 16 + k, 128, 32) if k else a("M", 16, 128, 32), a("BO", 0, 8, 16), True, False)
+            mm(a("B2", k, 8, 16), a("S", k, 128, 32) if k else a("M", 0, 128, 32), a("NIN"), False, True)
+        tt(a("VM"), a("B1", 0, 256), a("DM", 0, 256), A_.mult)
+        tt(a("VT"), a("B1", 0, 256), a("TRI"), A_.mult)
+        scan(a("CS"), a("SEGM", 0, 256), a("VM"), 0.0, A_.mult, A_.add)
+        tt(a("FSG"), a("B7", 0, 256), a("FA"), A_.mult)
+        tt(a("EE"), ind(a("CS"), a("L15")), a("VT"), A_.is_equal)
+        copy(a("GL"), a("CS", 15, 16, 16))
+        scan(a("ES"), a("SEGM", 0, 256), a("EE"), 0.0, A_.mult, A_.add)
+        ts(a("W1", 0, 16), a("ES", 15, 16, 16), -8192.0, A_.mult)
+        tt(a("W1", 16, 16), a("W1", 0, 16), a("CS", 15, 16, 16), A_.add)
+        tt(a("W1", 32, 16), a("W1", 16, 16), a("J0", 0, 16), A_.max)
+        copy(a("SL", 0, 16, 2), a("W1", 32, 16))
+        ts(a("GT"), a("B2", 0, 128), 0.0, A_.is_gt)
+        mm(a("B3", 256, 128), a("GT"), a("ID"), True, True)
+        tt(a("XN"), ind(a("W", 0, XB + V), a("GL")), a("FSG"), A_.add)
+        tt(a("PJ"), a("B3", 256, 128), a("DEO"), A_.mult)
+        tt(ind(a("JB"), a("JLU")), a("PJ"), a("LN", 0, 128, 2), A_.add)
+        first = route(topo, core, dst)
+        to = dst if first is None else first
+        need("G", None, [a("JB", 0, JW)], [])
+        rid, pid = topo.addr(to, core)
+        land = T[C][:, NP:CW] if first is None else T["RL%d" % t][:, 0:JW]
+        g.remote_dma(land, T.JB[:, 0:JW], T.sem["arr%d" % t] if first is None else T.sem["ra%d" % t], T.sem["ls%d" % t], pid, rid, emask(topo, core, to))
+        note("r%d" % t, [a("JB", 0, JW)], [], "ls%d" % t, 8, dict(known["G"]))
+        note("q%d" % t, [], [a(C, NP, JW)], "arr%d" % t, 8, {})
+        ts(a("XC"), a("XN"), 0.0, A_.max, 63.0, A_.min)
+        for b in range(15, -1, -1):
+            copy(ind(a("W", 0, XB + V), a("SL", 2 * b, 1)), a("XC", 16 * b, 16))
+        if t < RO - 1:
+            iota(a("LN", 0, LA), [[0, LA]], 2 * V, 0)
+            iota(a("LN", FB0, LF), [[0, LF]], 2 * V, 0)
+            order(t + 1)
+            negate(0, 1344, "V")
+        else:
+            dma("Y", T.yx[:], T.W[:, XB:XB + V], "st0", [a("W", XB, V)], [])
+        scan(a("M2", 2048, 1024), a("SEGM"), a("S2", 2048, 1024), 0.0, A_.mult, A_.max)
+        ts(a("FA2"), a("M2", 15, LF, 16), a("TT"), A_.is_lt)
+        mm(a("B6", 0, LF), a("BO"), a("FA2"), True, True)
+        act(a("YW", FB0, LF), a("B6", 0, LF), F_.Relu, -25.0, 8.0)
+        if t < RO - 1:
+            negate(1344, V - 1344, "S")
+            mm(a("B7", 256, 1), a("O32"), a("SGA"), True, True)
+            copy(a("AI", 0, 1), a("B7", 256, 1))
+            ts(a("AI", 1, 1), a("AI", 0, 1), 3, A_.bitwise_and)
+            tt(a("TT"), a("TH"), a("AI", 1, 1), A_.add)
+        tt(a("FW"), ind(a("YW"), a("PL", 0, Q)), a("DM"), A_.mult)
+        ts(a("NT"), a("DD"), a(C, NP + 128, 1), A_.is_ge)
+        tt(a("IXF", 0, Q), a("E0"), a("NT"), A_.mult)
+        tt(a("IXF", Q, Q), a("IXF", 0, Q), a("E1"), A_.add)
+        copy(a("IX", 0, Q), a("IXF", Q, Q))
+        act(a("C%d" % (t + 1), 0, NP), ind(a(C), a("IX", 0, Q)), F_.Identity)
+        scan(a("FWS"), a("SEGM", 0, NP), a("FW"), 0.0, A_.mult, A_.add)
+        tt(a("T1"), a("F1"), a("FWS", 15, Q, 16), A_.subtract)
+        tt(a("T2"), a("T1"), a("NT"), A_.mult)
+        if t < RO - 1:
+            lists(t + 1)
+    for i, (s0, p0, n) in enumerate(SEG):
+        dma("Y" if i % 2 else "S", T.yc[:, s0:s0 + n], T.C3[:, p0:p0 + n], "st%d" % (1 + i), [a("C3", p0, n)], [])
+    ts(a("FBB", 0, Q), a("T2"), 0.0, A_.max)
+    tt(a("FW"), ind(a("FBB"), a("LQ", 0, Q)), a("DM"), A_.mult)
+    mm(a("B4", 0, 512, p=8), a("BO", 0, 8, 16), a("FW", 0, 512), True, True)
+    mm(a("B6", 0, NP - 512, p=8), a("BO", 0, 8, 16), a("FW", 512, NP - 512), True, True)
+    for s0, p0, n in SEG:
+        n0 = max(0, min(n, 512 - p0))
+        if n0:
+            copy(a("YF8", s0, n0), a("B4", p0, n0, p=8))
+        if n > n0:
+            copy(a("YF8", s0 + n0, n - n0), a("B6", p0 + n0 - 512, n - n0, p=8))
+    dma("Y", T.yf[:], T.YF8[:], "st6", [a("YF8")], [])
+    for q in cnt:
+        g.wait_ge(T.sem["s" + q], cnt[q])
+    for i in range(4):
+        g.wait_ge(T.sem["ld%d" % i], 16)
+    for i in range(7):
+        g.wait_ge(T.sem["st%d" % i], 16)
+    for t in range(RO):
+        g.wait_ge(T.sem["ls%d" % t], 8)
+        g.wait_ge(T.sem["arr%d" % t], 8)

@@ -72,6 +72,71 @@ SEMAPHORES = ["sV", "sS", "sP", "sG"] + ["ld%d" % i for i in range(6)] + ["st%d"
     + ["arr%d" % i for i in range(RO)] + ["ls%d" % i for i in range(RO)] + ["ra%d" % i for i in range(RO)]
 
 
+CYC, GAT, SCA, WAKE, SLACK = 0.001, 1.5, 3.8, 0.1, 0.05
+PLAN = {}
+
+
+def plan(ops):
+    n = len(ops)
+    pred = [dict() for _ in range(n)]
+    succ = [[] for _ in range(n)]
+    hist, last = {}, {}
+    for i, (q, tag, reads, writes, occ, dur, _) in enumerate(ops):
+        for w, lst in ((False, reads), (True, writes)):
+            for _a, buf, m in lst:
+                ps = buf in SCRATCH and SCRATCH[buf][0] == "psum"
+                for em, ew, j in hist.get(buf, []):
+                    same = ops[j][1] == tag
+                    if j == i or (not (em & m and (w or ew)) and not ps) or (ps and same and q == "V" and not (em & m and (w or ew))):
+                        continue
+                    lat = 0.0 if same and (q == "P" or not ew) else WAKE
+                    if pred[i].get(j, -1.0) < lat:
+                        pred[i][j] = lat
+        for w, lst in ((False, reads), (True, writes)):
+            for _a, buf, m in lst:
+                h = hist.setdefault(buf, [])
+                ps = buf in SCRATCH and SCRATCH[buf][0] == "psum"
+                if w and not ps:
+                    h[:] = [e for e in h if e[0] & ~m or e[2] == i]
+                h.append((m, w, i))
+                if ps and len(h) > 150:
+                    h[:] = h[-150:]
+    for i in range(n):
+        for j, lat in pred[i].items():
+            succ[j].append((i, lat))
+    pr = [0.0] * n
+    for i in range(n - 1, -1, -1):
+        pr[i] = ops[i][5] + max([lat + pr[k] for k, lat in succ[i]] + [0.0])
+    left = [len(p) for p in pred]
+    est = [0.0] * n
+    ready, free = {}, {}
+    for i in range(n):
+        free[ops[i][0]] = 0.0
+        ready.setdefault(ops[i][0], [])
+        if not left[i]:
+            ready[ops[i][0]].append(i)
+    out = []
+    for _ in range(n):
+        best = None
+        for q in ready:
+            if ready[q]:
+                s0 = min(max(free[q], est[i]) for i in ready[q])
+                k = max((i for i in ready[q] if max(free[q], est[i]) <= s0 + SLACK), key=lambda i: (pr[i], -i))
+                s = max(free[q], est[k])
+                if best is None or s < best[0]:
+                    best = (s, q, k)
+        s, q, k = best
+        ready[q].remove(k)
+        free[q] = s + ops[k][4]
+        out.append(k)
+        for i, lat in succ[k]:
+            est[i] = max(est[i], s + ops[k][5] + lat)
+            left[i] -= 1
+            if not left[i]:
+                ready[ops[i][0]].append(i)
+    return out
+
+
 def route(topo, src, dst):
     if topo.may_write(src, dst):
         return None
@@ -174,63 +239,98 @@ def rank_program(g, core, T, topo):
             h[:] = [e for e in h if e[1] or e[2] != tag or e[0] & ~m]
             h.append((m, False, tag, sem, val, snap))
 
-    def run(q, fn, out, ins):
+    ops = []
+
+    def run(q, fn, out, ins, cost):
         writes = acc(out)[:1] if isinstance(out, tuple) else out
         reads = acc(out)[1:] if isinstance(out, tuple) else []
         for x in ins:
             reads = reads + acc(x)
-        need(q, q, reads, writes)
-        cnt[q] += 1
-        fn().then_inc(T.sem["s" + q], 1)
-        snap = dict(known[q])
-        snap["s" + q] = cnt[q]
-        note(q, reads, writes, "s" + q, cnt[q], snap)
+
+        def issue():
+            need(q, q, reads, writes)
+            cnt[q] += 1
+            fn().then_inc(T.sem["s" + q], 1)
+            snap = dict(known[q])
+            snap["s" + q] = cnt[q]
+            note(q, reads, writes, "s" + q, cnt[q], snap)
+        ops.append((q, q, reads, writes, cost, cost, issue))
 
     def dma(q, out, in_, sem, reads, writes):
-        need(q, None, reads, writes)
-        eng[q].dma_start(out, in_).then_inc(T.sem[sem], 16)
         serial[0] += 1
-        note("d%d" % serial[0], reads, writes, sem, 16, dict(known[q]))
+        tag = "d%d" % serial[0]
+
+        def issue():
+            need(q, None, reads, writes)
+            eng[q].dma_start(out, in_).then_inc(T.sem[sem], 16)
+            note(tag, reads, writes, sem, 16, dict(known[q]))
+        ops.append((q, tag, reads, writes, 0.05, 2.5, issue))
+
+    def cost(out, ins, per):
+        for x in ins:
+            if isinstance(x[1], tuple):
+                return 0.05 + GAT * CYC * 16 * bin(x[2][2]).count("1")
+        if isinstance(out[1], tuple):
+            return 0.05 + SCA * CYC * 16 * bin(out[2][2]).count("1")
+        two = all(SCRATCH[x[1]][2] in ("bfloat16", "uint16") for x in [out] + ins)
+        return CYC * max(64, bin(out[2]).count("1") * (per if per == 2 or not two else 0.5))
 
     def ap(x):
         return x[0]
 
     def copy(out, in_):
-        run("V", lambda: g.vector.tensor_copy(ap(out), ap(in_)), out, [in_])
+        run("V", lambda: g.vector.tensor_copy(ap(out), ap(in_)), out, [in_], cost(out, [in_], 1))
 
     def tt(out, x, y, op):
-        run("V", lambda: g.vector.tensor_tensor(ap(out), ap(x), ap(y), op), out, [x, y])
+        ps = any(isinstance(z[1], str) and SCRATCH[z[1]][0] == "psum" for z in (x, y))
+        run("V", lambda: g.vector.tensor_tensor(ap(out), ap(x), ap(y), op), out, [x, y], cost(out, [x, y], 1 if ps else 2))
 
     def ts(out, x, s1, op0, s2=None, op1=None):
         ins = [x] + [s for s in (s1, s2) if isinstance(s, tuple)]
         u1 = s1[0] if isinstance(s1, tuple) else s1
         if op1 is None:
-            run("V", lambda: g.vector.tensor_scalar(ap(out), ap(x), u1, None, op0), out, ins)
+            run("V", lambda: g.vector.tensor_scalar(ap(out), ap(x), u1, None, op0), out, ins, cost(out, [x], 1))
         else:
-            run("V", lambda: g.vector.tensor_scalar(ap(out), ap(x), u1, s2, op0, op1), out, ins)
+            run("V", lambda: g.vector.tensor_scalar(ap(out), ap(x), u1, s2, op0, op1), out, ins, cost(out, [x], 1))
 
     def scan(out, d0, d1, ini, op0, op1):
-        run("V", lambda: g.vector.tensor_tensor_scan(ap(out), ap(d0), ap(d1), ini, op0, op1), out, [d0, d1])
+        run("V", lambda: g.vector.tensor_tensor_scan(ap(out), ap(d0), ap(d1), ini, op0, op1), out, [d0, d1], cost(out, [d0, d1], 1))
 
     def fill(out, c):
-        run("V", lambda: g.vector.memset(ap(out), c), out, [])
+        run("V", lambda: g.vector.memset(ap(out), c), out, [], cost(out, [], 1))
 
     def act(out, x, func, bias=0.0, scale=1.0, accum=None):
         ins = [x] + ([bias] if isinstance(bias, tuple) else [])
         b = bias[0] if isinstance(bias, tuple) else bias
         if accum is None:
-            run("S", lambda: g.scalar.activation(ap(out), ap(x), func, bias=b, scale=scale), out, ins)
+            c = cost(out, [x], 2) if isinstance(x[1], tuple) else CYC * max(64, bin(out[2]).count("1"))
+            run("S", lambda: g.scalar.activation(ap(out), ap(x), func, bias=b, scale=scale), out, ins, c)
         else:
-            run("S", lambda: g.scalar.activation(ap(out), ap(x), func, bias=b, scale=scale, accum_out=ap(accum)), [out, accum], ins)
+            run("S", lambda: g.scalar.activation(ap(out), ap(x), func, bias=b, scale=scale, accum_out=ap(accum)), [out, accum], ins,
+                CYC * bin(out[2]).count("1"))
 
     def mm(out, l, r, start, stop):
-        run("P", lambda: g.tensor.matmul(ap(out), ap(l), ap(r), start, stop), out, [l, r])
+        c = CYC * max(min(64, bin(l[2]).count("1")), bin(r[2]).count("1")) * (4 if SCRATCH[l[1]][2] == "float32" else 1)
+        run("P", lambda: g.tensor.matmul(ap(out), ap(l), ap(r), start, stop), out, [l, r], c)
 
     def iota(out, pat, base, cm):
-        run("G", lambda: g.iota(ap(out), pat, base, cm, allow_small_or_imprecise_dtypes=True), out, [])
+        run("G", lambda: g.iota(ap(out), pat, base, cm, allow_small_or_imprecise_dtypes=True), out, [], 0.13 + 2 * CYC * bin(out[2]).count("1"))
 
     def sel(out, x, pat, op, fl, base, cm):
-        run("G", lambda: g.affine_select(ap(out), ap(x), pat, op, fl, base, cm), out, [x])
+        run("G", lambda: g.affine_select(ap(out), ap(x), pat, op, fl, base, cm), out, [x], 0.17 + 2 * CYC * bin(out[2]).count("1"))
+
+    def send(t, first, to, C):
+        src, net, land = a("JB", 0, JW), ("", "net", 1), a(C, NP, JW)
+
+        def issue():
+            need("G", None, [src], [])
+            rid, pid = topo.addr(to, core)
+            dst = T[C][:, NP:CW] if first is None else T["RL%d" % t][:, 0:JW]
+            g.remote_dma(dst, T.JB[:, 0:JW], T.sem["arr%d" % t] if first is None else T.sem["ra%d" % t], T.sem["ls%d" % t], pid, rid, emask(topo, core, to))
+            note("r%d" % t, [src], [], "ls%d" % t, 8, dict(known["G"]))
+        ops.append(("G", "r%d" % t, [src], [net], 0.3, 2.0, issue))
+        ops.append(("N", "q%d" % t, [net], [land], 0.0, 2.5 if first is None else 4.5,
+                    lambda: note("q%d" % t, [], [land], "arr%d" % t, 8, {})))
 
     dma("Y", T.FR[:], T.fr[:], "ld0", [], [a("FR")])
     dma("S", T.TI[:], T.th[:], "ld1", [], [a("TI")])
@@ -451,12 +551,7 @@ def rank_program(g, core, T, topo):
         tt(ind(a("JB"), a("JLU")), a("PJ"), a("LN", 0, 128, 2), A_.add)
         first = route(topo, core, dst)
         to = dst if first is None else first
-        need("G", None, [a("JB", 0, JW)], [])
-        rid, pid = topo.addr(to, core)
-        land = T[C][:, NP:CW] if first is None else T["RL%d" % t][:, 0:JW]
-        g.remote_dma(land, T.JB[:, 0:JW], T.sem["arr%d" % t] if first is None else T.sem["ra%d" % t], T.sem["ls%d" % t], pid, rid, emask(topo, core, to))
-        note("r%d" % t, [a("JB", 0, JW)], [], "ls%d" % t, 8, dict(known["G"]))
-        note("q%d" % t, [], [a(C, NP, JW)], "arr%d" % t, 8, {})
+        send(t, first, to, C)
         ts(a("XC"), a("XN"), 0.0, A_.max, 63.0, A_.min)
         for b in range(15, -1, -1):
             copy(ind(a("W", 0, XB + V), a("SL", 2 * b, 1)), a("XC", 16 * b, 16))
@@ -501,6 +596,10 @@ def rank_program(g, core, T, topo):
         if n > n0:
             copy(a("YF8", s0 + n0, n - n0), a("B6", p0 + n0 - 512, n - n0, p=8))
     dma("Y", T.yf[:], T.YF8[:], "st6", [a("YF8")], [])
+    if "order" not in PLAN:
+        PLAN["order"] = plan(ops)
+    for i in PLAN["order"]:
+        ops[i][6]()
     for q in cnt:
         g.wait_ge(T.sem["s" + q], cnt[q])
     for i in range(4):

@@ -17,9 +17,10 @@ SB = XB + 2 * V
 WW = SB + 16
 FB0 = K
 LW = 2 * K + NP
-JW = 132
+JW = 128
 CW = NP + JW
-JT = 136 + 128
+JT = JW + 128
+OFF = 64.0
 CH = 64
 NA, NF = LA // CH, LF // CH
 
@@ -31,7 +32,7 @@ SCRATCH = {
     "YW": ("sbuf", [128, LW], "bfloat16"), "OA": ("sbuf", [128, LA], "uint16"), "OF": ("sbuf", [128, LF], "uint16"),
     "FR": ("sbuf", [8, K], "int32"), "FRB": ("sbuf", [8, NP], "bfloat16"), "TI": ("sbuf", [128, 1], "int32"),
     "TH": ("sbuf", [128, 1], "float32"), "TT": ("sbuf", [128, 1], "float32"), "AI": ("sbuf", [128, 2], "int32"),
-    "ONE": ("sbuf", [128, NP], "bfloat16"), "PM": ("sbuf", [16, NP], "bfloat16"), "QM": ("sbuf", [8, 128], "bfloat16"),
+    "ONE": ("sbuf", [128, NP], "bfloat16"), "PM": ("sbuf", [16, 416], "bfloat16"), "QM": ("sbuf", [8, 128], "bfloat16"),
     "QM0": ("sbuf", [8, 128], "bfloat16"), "LT": ("sbuf", [16, 256], "bfloat16"), "ID": ("sbuf", [128, 128], "bfloat16"),
     "DM": ("sbuf", [128, NP], "bfloat16"), "TRI": ("sbuf", [128, 256], "bfloat16"), "BO": ("sbuf", [128, 128], "bfloat16"),
     "BOF": ("sbuf", [128, 128], "float32"), "TS": ("sbuf", [128, 128], "bfloat16"), "SH": ("sbuf", [128, 128], "float32"),
@@ -49,8 +50,9 @@ SCRATCH = {
     "FW": ("sbuf", [128, NP], "bfloat16"), "FWS": ("sbuf", [128, NP], "bfloat16"), "FL": ("sbuf", [128, 3 * Q], "bfloat16"),
     "GE": ("sbuf", [128, Q], "bfloat16"), "O1": ("sbuf", [2 * Q, 128], "bfloat16"), "O2": ("sbuf", [Q, 128], "bfloat16"),
     "MM": ("sbuf", [128, 2 * Q], "float32"), "PS": ("sbuf", [128, 2 * Q], "float32"), "PL": ("sbuf", [128, 52], "uint16"),
-    "F1": ("sbuf", [128, Q], "float32"), "DD": ("sbuf", [128, Q], "float32"), "E0": ("sbuf", [128, Q], "float32"),
-    "E1": ("sbuf", [128, Q], "float32"), "NT": ("sbuf", [128, Q], "float32"), "IXF": ("sbuf", [128, 2 * Q], "float32"),
+    "F1": ("sbuf", [128, Q], "float32"), "DD": ("sbuf", [128, Q], "float32"), "EN": ("sbuf", [128, 3 * Q], "float32"), "LX": ("sbuf", [128, LA], "float32"),
+    "NN": ("sbuf", [128, 4], "float32"), "RN": ("sbuf", [128, 4], "float32"),
+    "IXF": ("sbuf", [128, 2 * Q], "float32"),
     "IX": ("sbuf", [128, 52], "uint16"), "FA": ("sbuf", [128, LA], "bfloat16"), "FA2": ("sbuf", [128, LF], "bfloat16"),
     "VV": ("sbuf", [128, LA], "bfloat16"), "SG": ("sbuf", [128, LA], "bfloat16"), "DLV": ("sbuf", [128, LA], "float32"),
     "DLS": ("sbuf", [128, LA], "bfloat16"), "DEO": ("sbuf", [128, 128], "float32"), "VI": ("sbuf", [128, LA], "bfloat16"),
@@ -63,17 +65,20 @@ SCRATCH = {
     "SL": ("sbuf", [128, 32], "uint16"), "FSG": ("sbuf", [128, 256], "float32"), "XN": ("sbuf", [128, 256], "bfloat16"),
     "XC": ("sbuf", [128, 256], "bfloat16"), "GT": ("sbuf", [128, 128], "bfloat16"), "PJ": ("sbuf", [128, 128], "float32"),
     "JB": ("sbuf", [128, JT], "float32"), "SGA": ("sbuf", [128, 1], "float32"), "SGJ": ("sbuf", [128, LA], "float32"),
-    "YF8": ("sbuf", [8, K], "float32"), "FBB": ("sbuf", [128, 64], "bfloat16"),
-    "RL0": ("sbuf", [128, JW], "float32"), "RL2": ("sbuf", [128, JW], "float32"),
+    "YF8": ("sbuf", [8, NP], "float32"), "FBB": ("sbuf", [128, 64], "bfloat16"),
+    "RL": ("sbuf", [128, RO * JW], "float32"),
 }
 for _i in range(8):
     SCRATCH["B%d" % _i] = ("psum", [128, 512], "float32")
 SEMAPHORES = ["sV", "sS", "sP", "sG"] + ["ld%d" % i for i in range(6)] + ["st%d" % i for i in range(14)] \
-    + ["arr%d" % i for i in range(RO)] + ["ls%d" % i for i in range(RO)] + ["ra%d" % i for i in range(RO)]
+    + [s + str(i) for s in ("arr", "ls", "ra", "na", "nl", "rn") for i in range(RO)]
 
 
-CYC, GAT, SCA, WAKE, SLACK = 0.001, 1.5, 3.8, 0.1, 0.05
+CYC, GAT, SCA, WAKE, SLACK = 0.001, 1.5, 3.8, 0.15, 0.1
 PLAN = {}
+SEED = [8067, 0.3]
+QW = {"V": 1.0, "S": 1.0, "P": 1.0, "G": 1.0, "Y": 1.0, "N": 1.0}
+NEGV = V
 
 
 def plan(ops):
@@ -106,7 +111,9 @@ def plan(ops):
             succ[j].append((i, lat))
     pr = [0.0] * n
     for i in range(n - 1, -1, -1):
-        pr[i] = ops[i][5] + max([lat + pr[k] for k, lat in succ[i]] + [0.0])
+        pr[i] = ops[i][5] * QW[ops[i][0]] + max([lat + pr[k] for k, lat in succ[i]] + [0.0])
+    if SEED[0]:
+        pr = [float(x) for x in np.array(pr) + SEED[1] * np.random.default_rng(SEED[0]).random(n)]
     left = [len(p) for p in pred]
     est = [0.0] * n
     ready, free = {}, {}
@@ -158,12 +165,15 @@ def relay_program(g, core, T, topo):
             dst = T.cores[(r + 1 + t % 3) % N]
             if route(topo, src, dst) == core:
                 rid, pid = topo.addr(dst, core)
-                buf = T["RL%d" % t]
+                m = emask(topo, core, dst)
+                g.wait_ge(T.sem["rn%d" % t], 8)
+                g.remote_dma(T.NN[:, t:t + 1], T.RN[:, t:t + 1], T.sem["na%d" % t], T.sem["nl%d" % t], pid, rid, m)
                 g.wait_ge(T.sem["ra%d" % t], 8)
-                g.remote_dma(T["C%d" % t][:, NP:CW], buf[:, 0:JW], T.sem["arr%d" % t], T.sem["ls%d" % t], pid, rid, emask(topo, core, dst))
+                g.remote_dma(T["C%d" % t][:, NP:CW], T.RL[:, t * JW:(t + 1) * JW], T.sem["arr%d" % t], T.sem["ls%d" % t], pid, rid, m)
     for r in range(N):
         for t in range(RO):
             if route(topo, T.cores[r], T.cores[(r + 1 + t % 3) % N]) == core:
+                g.wait_ge(T.sem["nl%d" % t], 8)
                 g.wait_ge(T.sem["ls%d" % t], 8)
 
 
@@ -256,7 +266,7 @@ def rank_program(g, core, T, topo):
             note(q, reads, writes, "s" + q, cnt[q], snap)
         ops.append((q, q, reads, writes, cost, cost, issue))
 
-    def dma(q, out, in_, sem, reads, writes):
+    def dma(q, out, in_, sem, reads, writes, dur=2.5):
         serial[0] += 1
         tag = "d%d" % serial[0]
 
@@ -264,7 +274,7 @@ def rank_program(g, core, T, topo):
             need(q, None, reads, writes)
             eng[q].dma_start(out, in_).then_inc(T.sem[sem], 16)
             note(tag, reads, writes, sem, 16, dict(known[q]))
-        ops.append((q, tag, reads, writes, 0.05, 2.5, issue))
+        ops.append((q, tag, reads, writes, 0.05, dur, issue))
 
     def cost(out, ins, per):
         for x in ins:
@@ -303,6 +313,9 @@ def rank_program(g, core, T, topo):
         ins = [x] + ([bias] if isinstance(bias, tuple) else [])
         b = bias[0] if isinstance(bias, tuple) else bias
         if accum is None:
+            if isinstance(out[1], tuple):
+                run("S", lambda: g.scalar.activation(ap(out), ap(x), func), out, ins, cost(out, [x], 1))
+                return
             c = cost(out, [x], 2) if isinstance(x[1], tuple) else CYC * max(64, bin(out[2]).count("1"))
             run("S", lambda: g.scalar.activation(ap(out), ap(x), func, bias=b, scale=scale), out, ins, c)
         else:
@@ -319,36 +332,41 @@ def rank_program(g, core, T, topo):
     def sel(out, x, pat, op, fl, base, cm):
         run("G", lambda: g.affine_select(ap(out), ap(x), pat, op, fl, base, cm), out, [x], 0.17 + 2 * CYC * bin(out[2]).count("1"))
 
-    def send(t, first, to, C):
-        src, net, land = a("JB", 0, JW), ("", "net", 1), a(C, NP, JW)
+    def send(t, src, land, relay, arr, ra, ls, lat):
+        dst = T.cores[(rank + 1 + t % 3) % N]
+        first = route(topo, core, dst)
+        to = dst if first is None else first
+        net = ("", "net" + arr, 1)
 
         def issue():
             need("G", None, [src], [])
             rid, pid = topo.addr(to, core)
-            dst = T[C][:, NP:CW] if first is None else T["RL%d" % t][:, 0:JW]
-            g.remote_dma(dst, T.JB[:, 0:JW], T.sem["arr%d" % t] if first is None else T.sem["ra%d" % t], T.sem["ls%d" % t], pid, rid, emask(topo, core, to))
-            note("r%d" % t, [src], [], "ls%d" % t, 8, dict(known["G"]))
-        ops.append(("G", "r%d" % t, [src], [net], 0.3, 2.0, issue))
-        ops.append(("N", "q%d" % t, [net], [land], 0.0, 2.5 if first is None else 4.5,
-                    lambda: note("q%d" % t, [], [land], "arr%d" % t, 8, {})))
+            g.remote_dma(land[0] if first is None else relay, src[0], T.sem[(arr if first is None else ra) + str(t)], T.sem[ls + str(t)],
+                         pid, rid, emask(topo, core, to))
+            note("r%s%d" % (ls, t), [src], [], ls + str(t), 8, dict(known["G"]))
+        ops.append(("G", "r%s%d" % (ls, t), [src], [net], 0.3, 2.0, issue))
+        ops.append(("N", "q%s%d" % (arr, t), [net], [land], 0.0, lat * (1 if first is None else 2),
+                    lambda: note("q%s%d" % (arr, t), [], [land], arr + str(t), 8, {})))
 
-    dma("Y", T.FR[:], T.fr[:], "ld0", [], [a("FR")])
-    dma("S", T.TI[:], T.th[:], "ld1", [], [a("TI")])
-    dma("Y", T.CI[:], T.cl[:], "ld2", [], [a("CI")])
-    dma("S", T.W[:, XB:XB + V], T.xv[:], "ld3", [], [a("W", XB, V)])
+    dma("Y", T.FR[:], T.fr[:], "ld0", [], [a("FR")], 2.2)
+    dma("Y", T.CI[:], T.cl[:], "ld2", [], [a("CI")], 4.0)
+    dma("Y", T.W[:, XB:XB + V], T.xv[:], "ld3", [], [a("W", XB, V)], 6.0)
+    dma("Y", T.TI[:], T.th[:], "ld1", [], [a("TI")], 6.0)
+    fill(a("VM", 0, 16), 200.0)
+    act(a("W", SB, 16), a("VM", 0, 16), F_.Silu)
 
     fill(a("ONE"), 1.0)
     fill(a("FRB"), 8.0)
-    sel(a("PM"), a("ONE", p=16), [[0, Q], [1, 16]], A_.is_equal, 0.0, 0, -1)
+    sel(a("PM"), a("ONE", 0, 416, p=16), [[0, 26], [1, 16]], A_.is_equal, 0.0, 0, -1)
     sel(a("QM0"), a("ONE", 0, 128, p=8), [[1, 128]], A_.is_ge, 0.0, 0, -16)
     sel(a("QM"), a("QM0"), [[-1, 128]], A_.is_ge, 0.0, 15, 16)
     fill(a("SEGM"), 1.0)
     fill(a("SEGM", 0, 64, 16), 0.0)
-    mm(a("B1", 0, 512), a("PM", 0, 128), a("PM", 0, 512), True, True)
-    mm(a("B2", 0, NP - 512), a("PM", 0, 128), a("PM", 512, NP - 512), True, True)
+    mm(a("B1", 0, 416), a("PM", 0, 128), a("PM", 0, 416), True, True)
+    mm(a("B2", 0, NP - 416), a("PM", 0, 128), a("PM", 0, NP - 416), True, True)
     mm(a("B3", 0, 128), a("QM"), a("QM"), True, True)
-    copy(a("DM", 0, 512), a("B1", 0, 512))
-    copy(a("DM", 512, NP - 512), a("B2", 0, NP - 512))
+    copy(a("DM", 0, 416), a("B1", 0, 416))
+    act(a("DM", 416, NP - 416), a("B2", 0, NP - 416), F_.Identity)
     copy(a("BO"), a("B3", 0, 128))
     for s0, p0, n in SEG:
         copy(a("FRB", p0, n), a("FR", s0, n))
@@ -383,9 +401,9 @@ def rank_program(g, core, T, topo):
     mm(a("B6", 0, Q), a("CL"), a("CR", 0, Q), True, True)
     ts(a("PD"), a("B6", 0, Q), -1.0, A_.mult)
     ts(a("J0"), a("PD"), -2.0 * K, A_.add)
-    ts(a("JD"), a("J0", 0, 8), 136.0 - 512.0, A_.add)
-    iota(a("LN", 0, LA), [[0, LA]], 2 * V, 0)
-    iota(a("LN", FB0, LF), [[0, LF]], 2 * V, 0)
+    ts(a("JD"), a("J0", 0, 8), float(JW - 512), A_.add)
+    iota(a("LN", 0, LA), [[0, LA]], 2 * V + int(OFF), 0)
+    iota(a("LN", FB0, LF), [[0, LF]], 2 * V + int(OFF), 0)
 
     def lists(t):
         ts(a("FL", 0, Q), a("T2"), 0.0, A_.is_le)
@@ -402,8 +420,9 @@ def rank_program(g, core, T, topo):
         tt(a("PS", 0, Q), a("MM", 0, Q), a("MM", Q, Q), A_.add)
         tt(a("PS", Q, Q), a("PS", 0, Q), a("PD"), A_.add)
         copy(a("PL", 0, Q), a("PS", Q, Q))
-        copy(ind(a("LN"), a("PL", 0, Q)), a("C%d" % t, 0, NP))
-        copy(a("OA"), a("LN", 0, LA))
+        act(ind(a("LN"), a("PL", 0, Q)), a("C%d" % t, 0, NP), F_.Silu)
+        ts(a("OA"), a("LN", 0, LA), 0.25 - OFF, A_.add)
+        ts(a("OF"), a("LN", FB0, LF), 0.25 - OFF, A_.add)
         mm(a("B5", 0, 128, p=Q), a("FL", 2 * Q, Q), a("BO"), True, True)
         act(a("O2"), a("B5", 0, 128, p=Q), F_.Identity)
         mm(a("B5", 128, Q), a("TS"), a("FL", 2 * Q, Q), True, False)
@@ -424,14 +443,12 @@ def rank_program(g, core, T, topo):
             act(a("W", XB + V + lo, n), a("W", XB + lo, n), F_.Identity, 63.0, -1.0)
 
     for s0, p0, n in SEG:
-        fill(a("C0", p0 + n, -(-n // 16) * 16 - n), 0.0)
-        copy(a("C0", p0, n), a("CI", s0, n))
+        fill(a("C0", p0 + n, -(-n // 16) * 16 - n), OFF)
+        ts(a("C0", p0, n), a("CI", s0, n), OFF, A_.add)
     sel(a("ID"), a("ONE", 0, 128), [[-1, 128]], A_.is_equal, 0.0, 0, 1)
     ts(a("NI4"), a("ID"), -4096.0, A_.mult)
     lists(0)
-    negate(0, 1344, "V")
-    negate(1344, V - 1344, "S")
-    fill(a("W", SB, 16), 200.0)
+    negate(0, V, "S")
     fill(a("W", 0, XB), 0.0)
     fill(a("RST"), 64.0)
     fill(a("RST", 0, 64, 16), 8192.0)
@@ -455,7 +472,7 @@ def rank_program(g, core, T, topo):
     ts(a("I4"), a("ID"), 4096.0, A_.mult)
     ts(a("I16"), a("BO", 0, 8, 16), 16.0, A_.mult)
     ts(a("NIN"), a("BO", 0, 8, 16), -1.0, A_.mult)
-    ts(a("KV"), a("DM", 15, 1), float(XB - V // 2 - 4096), A_.mult)
+    ts(a("KV"), a("DM", 15, 1), float(XB - V // 2 - 4096 - OFF), A_.mult)
     iota(a("KC0"), [[0, 16], [-16384, 16]], 262144, 0)
     iota(a("KC1"), [[0, 16], [-1, 16]], 15, 0)
     iota(a("KW"), [[0, 8], [1024, 16]], -16384, 0)
@@ -469,20 +486,19 @@ def rank_program(g, core, T, topo):
     act(a("TRI"), a("B4", 0, 256), F_.Identity)
 
     for t in range(RO):
-        dst = T.cores[(rank + 1 + t % 3) % N]
         C = "C%d" % t
         gather("S", 0, "S", "OA")
         gather("V", 1, "S", "OA")
         gather("S", 2, "S", "OA")
         gather("S", 3, "S", "OA")
-        copy(a("OF"), a("LN", FB0, LF))
-        tt(a("DEO"), a("LN", 1, 128, 2), a("LN", 0, 128, 2), A_.subtract)
+        ts(a("LX"), a("OA"), OFF, A_.add)
+        tt(a("DEO"), a("LX", 1, 128, 2), a("LX", 0, 128, 2), A_.subtract)
         tt(a("DD"), a("B5", 128, Q), a("DC"), A_.add)
-        ts(a("E1"), a("DD"), 513.0 + NP, A_.add)
-        tt(a("E0"), a("J0"), a("E1"), A_.subtract)
-        act(a("SG"), a("LN", 0, LA), F_.Sign, 0.5 - V)
+        ts(a("EN", Q, Q), a("DD"), 513.0 + NP, A_.add)
+        tt(a("EN", 0, Q), a("J0"), a("EN", Q, Q), A_.subtract)
+        act(a("SG"), a("LN", 0, LA), F_.Sign, 0.5 - V - OFF)
         for h in range(2):
-            mm(a("B2", 128 * h, 128), a("DF"), a("LN", h, 128, 2), True, False)
+            mm(a("B2", 128 * h, 128), a("DF"), a("LX", h, 128, 2), True, False)
             mm(a("B2", 128 * h, 128), a("D1024"), a("SG", h, 128, 2), False, True)
             mm(a("B2", 256 + 128 * h, 128), a("D8"), a("SG", h, 128, 2), True, True)
         act(a("DLV"), a("B2", 0, 256), F_.Identity, a("KV"))
@@ -515,7 +531,7 @@ def rank_program(g, core, T, topo):
         scan(a("IS"), a("SEGM", 0, 128), a("IBD"), 0.0, A_.mult, A_.add)
         tt(a("JL"), a("IS", 15, 8, 16), a("JD"), A_.min)
         ts(a("JLU"), a("JL"), 512.0, A_.add)
-        copy(a("JB", 128, 1), a("INC", 127, 1))
+        send(t, a("INC", 127, 1), a("NN", t, 1), T.RN[:, t:t + 1], "na", "rn", "nl", 2.0)
         scan(a("R"), a("SEGM", 0, 256), a("B0", 0, 256), 0.0, A_.mult, A_.max)
         scan(a("VT"), a("SEGM", 0, 256), a("B0", 0, 256), 0.0, A_.mult, A_.max)
         tt(a("EQ"), ind(a("R"), a("L15")), a("VT"), A_.is_equal)
@@ -548,39 +564,39 @@ def rank_program(g, core, T, topo):
         mm(a("B3", 256, 128), a("GT"), a("ID"), True, True)
         tt(a("XN"), ind(a("W", 0, XB + V), a("GL")), a("FSG"), A_.add)
         tt(a("PJ"), a("B3", 256, 128), a("DEO"), A_.mult)
-        tt(ind(a("JB"), a("JLU")), a("PJ"), a("LN", 0, 128, 2), A_.add)
-        first = route(topo, core, dst)
-        to = dst if first is None else first
-        send(t, first, to, C)
+        tt(ind(a("JB"), a("JLU")), a("PJ"), a("LX", 0, 128, 2), A_.add)
+        send(t, a("JB", 0, JW), a(C, NP, JW), T.RL[:, t * JW:(t + 1) * JW], "arr", "ra", "ls", 2.2)
         ts(a("XC"), a("XN"), 0.0, A_.max, 63.0, A_.min)
         for b in range(15, -1, -1):
             copy(ind(a("W", 0, XB + V), a("SL", 2 * b, 1)), a("XC", 16 * b, 16))
         if t < RO - 1:
-            iota(a("LN", 0, LA), [[0, LA]], 2 * V, 0)
-            iota(a("LN", FB0, LF), [[0, LF]], 2 * V, 0)
+            iota(a("LN", 0, LA), [[0, LA]], 2 * V + int(OFF), 0)
+            iota(a("LN", FB0, LF), [[0, LF]], 2 * V + int(OFF), 0)
             order(t + 1)
-            negate(0, 1344, "V")
+            if NEGV:
+                negate(0, NEGV, "V")
+            if NEGV < V:
+                negate(NEGV, V - NEGV, "S")
         else:
-            dma("Y", T.yx[:], T.W[:, XB:XB + V], "st0", [a("W", XB, V)], [])
+            dma("Y", T.yx[:], T.W[:, XB:XB + V], "st0", [a("W", XB, V)], [], 4.5)
         scan(a("M2", 2048, 1024), a("SEGM"), a("S2", 2048, 1024), 0.0, A_.mult, A_.max)
         ts(a("FA2"), a("M2", 15, LF, 16), a("TT"), A_.is_lt)
         mm(a("B6", 0, LF), a("BO"), a("FA2"), True, True)
         act(a("YW", FB0, LF), a("B6", 0, LF), F_.Relu, -25.0, 8.0)
         if t < RO - 1:
-            negate(1344, V - 1344, "S")
             mm(a("B7", 256, 1), a("O32"), a("SGA"), True, True)
             copy(a("AI", 0, 1), a("B7", 256, 1))
             ts(a("AI", 1, 1), a("AI", 0, 1), 3, A_.bitwise_and)
             tt(a("TT"), a("TH"), a("AI", 1, 1), A_.add)
         tt(a("FW"), ind(a("YW"), a("PL", 0, Q)), a("DM"), A_.mult)
-        ts(a("NT"), a("DD"), a(C, NP + 128, 1), A_.is_ge)
-        tt(a("IXF", 0, Q), a("E0"), a("NT"), A_.mult)
-        tt(a("IXF", Q, Q), a("IXF", 0, Q), a("E1"), A_.add)
+        ts(a("EN", 2 * Q, Q), a("DD"), a("NN", t, 1), A_.is_ge)
+        tt(a("IXF", 0, Q), a("EN", 0, Q), a("EN", 2 * Q, Q), A_.mult)
+        tt(a("IXF", Q, Q), a("IXF", 0, Q), a("EN", Q, Q), A_.add)
         copy(a("IX", 0, Q), a("IXF", Q, Q))
-        act(a("C%d" % (t + 1), 0, NP), ind(a(C), a("IX", 0, Q)), F_.Identity)
+        act(a("C%d" % (t + 1), 0, NP), ind(a(C), a("IX", 0, Q)), F_.Identity, -OFF if t == RO - 1 else 0.0)
         scan(a("FWS"), a("SEGM", 0, NP), a("FW"), 0.0, A_.mult, A_.add)
         tt(a("T1"), a("F1"), a("FWS", 15, Q, 16), A_.subtract)
-        tt(a("T2"), a("T1"), a("NT"), A_.mult)
+        tt(a("T2"), a("T1"), a("EN", 2 * Q, Q), A_.mult)
         if t < RO - 1:
             lists(t + 1)
     for i, (s0, p0, n) in enumerate(SEG):
@@ -589,13 +605,10 @@ def rank_program(g, core, T, topo):
     tt(a("FW"), ind(a("FBB"), a("LQ", 0, Q)), a("DM"), A_.mult)
     mm(a("B4", 0, 512, p=8), a("BO", 0, 8, 16), a("FW", 0, 512), True, True)
     mm(a("B6", 0, NP - 512, p=8), a("BO", 0, 8, 16), a("FW", 512, NP - 512), True, True)
-    for s0, p0, n in SEG:
-        n0 = max(0, min(n, 512 - p0))
-        if n0:
-            copy(a("YF8", s0, n0), a("B4", p0, n0, p=8))
-        if n > n0:
-            copy(a("YF8", s0 + n0, n - n0), a("B6", p0 + n0 - 512, n - n0, p=8))
-    dma("Y", T.yf[:], T.YF8[:], "st6", [a("YF8")], [])
+    act(a("YF8", 0, 512), a("B4", 0, 512, p=8), F_.Identity)
+    copy(a("YF8", 512, NP - 512), a("B6", 0, NP - 512, p=8))
+    for i, (s0, p0, n) in enumerate(SEG):
+        dma("Y" if i % 2 else "S", T.yf[:, s0:s0 + n], T.YF8[:, p0:p0 + n], "st%d" % (6 + i), [a("YF8", p0, n)], [])
     if "order" not in PLAN:
         PLAN["order"] = plan(ops)
     for i in PLAN["order"]:
@@ -604,8 +617,8 @@ def rank_program(g, core, T, topo):
         g.wait_ge(T.sem["s" + q], cnt[q])
     for i in range(4):
         g.wait_ge(T.sem["ld%d" % i], 16)
-    for i in range(7):
+    for i in range(11):
         g.wait_ge(T.sem["st%d" % i], 16)
     for t in range(RO):
-        g.wait_ge(T.sem["ls%d" % t], 8)
-        g.wait_ge(T.sem["arr%d" % t], 8)
+        for s in ("ls", "arr", "nl", "na"):
+            g.wait_ge(T.sem[s + str(t)], 8)

import numpy as np
from concourse.mybir import dt, AluOpType, AxisListType, ActivationFunctionType

A_, F_ = AluOpType, ActivationFunctionType
N, V, K, LA, LF, RO, AS, FS = 8, 2048, 768, 256, 192, 3, 170, 255
BRK = sorted(set([0] + [AS * t % K for t in range(RO)] + [FS * t % K for t in range(RO)])) + [K]
SEG = []
_p = 0
for _a, _b in zip(BRK[:-1], BRK[1:]):
    SEG.append((_a, _p, _b - _a))
    _p += -(-(_b - _a) // 16) * 16
NP = _p
Q = NP // 16
START = {a: p // 16 for a, p, n in SEG}
XB = 256
SB = XB + 2 * V
WW = SB + 16
FB0 = K
LW = 2 * K + NP
JW = 128
CW = NP + JW
JT = JW + 128
OFF = 64.0
CH = 64
NA, NF = LA // CH, LF // CH

SCRATCH = {
    "W": ("sbuf", [128, WW], "bfloat16"), "S": ("sbuf", [128, 16 * LA], "bfloat16"), "M": ("sbuf", [128, 16 * LA], "bfloat16"),
    "Z": ("sbuf", [128, 16 * LA], "bfloat16"), "S2": ("sbuf", [128, 16 * LF], "bfloat16"), "M2": ("sbuf", [128, 16 * LF], "bfloat16"),
    "C0": ("sbuf", [128, CW], "float32"), "C1": ("sbuf", [128, CW], "float32"), "C2": ("sbuf", [128, CW], "float32"),
    "C3": ("sbuf", [128, CW], "float32"), "CI": ("sbuf", [128, K], "int32"), "LN": ("sbuf", [128, LW], "float32"),
    "YW": ("sbuf", [128, LW], "bfloat16"), "OA": ("sbuf", [128, LA], "uint16"), "OF": ("sbuf", [128, LF], "uint16"),
    "FR": ("sbuf", [8, K], "int32"), "FRB": ("sbuf", [8, NP], "bfloat16"), "TI": ("sbuf", [128, 1], "int32"),
    "TH": ("sbuf", [128, 1], "float32"), "TT": ("sbuf", [128, 1], "float32"), "AI": ("sbuf", [128, 2], "int32"),
    "ONE": ("sbuf", [128, NP], "bfloat16"), "PM": ("sbuf", [16, 416], "bfloat16"), "QM": ("sbuf", [8, 128], "bfloat16"),
    "QM0": ("sbuf", [8, 128], "bfloat16"), "LT": ("sbuf", [16, 256], "bfloat16"), "ID": ("sbuf", [128, 128], "bfloat16"),
    "DM": ("sbuf", [128, NP], "bfloat16"), "TRI": ("sbuf", [128, 256], "bfloat16"), "BO": ("sbuf", [128, 128], "bfloat16"),
    "BOF": ("sbuf", [128, 128], "float32"), "TS": ("sbuf", [128, 128], "bfloat16"), "SH": ("sbuf", [128, 128], "float32"),
    "DF": ("sbuf", [128, 128], "float32"), "D1024": ("sbuf", [128, 128], "bfloat16"), "D8": ("sbuf", [128, 128], "bfloat16"),
    "I4": ("sbuf", [128, 128], "bfloat16"), "NI4": ("sbuf", [128, 128], "bfloat16"), "I16": ("sbuf", [128, 8], "bfloat16"),
    "NIN": ("sbuf", [128, 8], "bfloat16"), "O32": ("sbuf", [128, 128], "float32"), "KV": ("sbuf", [128, 1], "float32"),
    "KC0": ("sbuf", [1, 256], "bfloat16"), "KC1": ("sbuf", [1, 256], "bfloat16"), "KW": ("sbuf", [128, 128], "bfloat16"),
    "WC": ("sbuf", [128, 128], "bfloat16"), "L15": ("sbuf", [128, 16], "uint16"),
    "LQI": ("sbuf", [128, 68], "int32"), "LQ": ("sbuf", [128, 52], "uint16"), "CL0": ("sbuf", [2, 128], "bfloat16"),
    "CL": ("sbuf", [2, 128], "bfloat16"), "CR0": ("sbuf", [2, 2 * Q], "bfloat16"), "CR": ("sbuf", [2, 2 * Q], "bfloat16"),
    "PD": ("sbuf", [128, Q], "float32"), "J0": ("sbuf", [128, Q], "float32"), "JD": ("sbuf", [128, 8], "float32"),
    "U0": ("sbuf", [2 * Q, 2 * Q], "bfloat16"), "U1": ("sbuf", [2 * Q, 2 * Q], "bfloat16"), "U2": ("sbuf", [2 * Q, 2 * Q], "bfloat16"),
    "UT": ("sbuf", [2 * Q, 2 * Q], "bfloat16"), "SEGM": ("sbuf", [128, 1024], "bfloat16"), "RST": ("sbuf", [128, 1024], "bfloat16"),
    "DC": ("sbuf", [128, Q], "float32"), "T2": ("sbuf", [128, Q], "float32"), "T1": ("sbuf", [128, Q], "float32"),
    "FW": ("sbuf", [128, NP], "bfloat16"), "FWS": ("sbuf", [128, NP], "bfloat16"), "FL": ("sbuf", [128, 3 * Q], "bfloat16"),
    "GE": ("sbuf", [128, Q], "bfloat16"), "O1": ("sbuf", [2 * Q, 128], "bfloat16"), "O2": ("sbuf", [Q, 128], "bfloat16"),
    "MM": ("sbuf", [128, 2 * Q], "float32"), "PS": ("sbuf", [128, 2 * Q], "float32"), "PL": ("sbuf", [128, 52], "uint16"),
    "F1": ("sbuf", [128, Q], "float32"), "DD": ("sbuf", [128, Q], "float32"), "EN": ("sbuf", [128, 3 * Q], "float32"), "LX": ("sbuf", [128, LA], "float32"),
    "NN": ("sbuf", [128, 4], "float32"), "RN": ("sbuf", [128, 4], "float32"),
    "IXF": ("sbuf", [128, 2 * Q], "float32"),
    "IX": ("sbuf", [128, 52], "uint16"), "FA": ("sbuf", [128, LA], "bfloat16"), "FA2": ("sbuf", [128, LF], "bfloat16"),
    "VV": ("sbuf", [128, LA], "bfloat16"), "SG": ("sbuf", [128, LA], "bfloat16"), "DLV": ("sbuf", [128, LA], "float32"),
    "DLS": ("sbuf", [128, LA], "bfloat16"), "DEO": ("sbuf", [128, 128], "float32"), "VI": ("sbuf", [128, LA], "bfloat16"),
    "BT": ("sbuf", [128, 128], "bfloat16"), "INC": ("sbuf", [128, 128], "float32"), "IB": ("sbuf", [128, 128], "float32"),
    "IBD": ("sbuf", [128, 128], "float32"), "IS": ("sbuf", [128, 128], "float32"), "JL": ("sbuf", [128, 8], "float32"),
    "JLU": ("sbuf", [128, 8], "uint16"), "R": ("sbuf", [128, 256], "float32"), "EQ": ("sbuf", [128, 256], "bfloat16"),
    "HV": ("sbuf", [128, 256], "float32"), "HS": ("sbuf", [128, 256], "bfloat16"), "VM": ("sbuf", [128, 256], "float32"),
    "CS": ("sbuf", [128, 256], "float32"), "GL": ("sbuf", [128, 16], "uint16"), "VT": ("sbuf", [128, 256], "float32"),
    "EE": ("sbuf", [128, 256], "bfloat16"), "ES": ("sbuf", [128, 256], "bfloat16"), "W1": ("sbuf", [128, 48], "float32"),
    "SL": ("sbuf", [128, 32], "uint16"), "FSG": ("sbuf", [128, 256], "float32"), "XN": ("sbuf", [128, 256], "bfloat16"),
    "XC": ("sbuf", [128, 256], "bfloat16"), "GT": ("sbuf", [128, 128], "bfloat16"), "PJ": ("sbuf", [128, 128], "float32"),
    "JB": ("sbuf", [128, JT], "float32"), "SGA": ("sbuf", [128, 1], "float32"), "SGJ": ("sbuf", [128, LA], "float32"),
    "YF8": ("sbuf", [8, NP], "float32"), "FBB": ("sbuf", [128, 64], "bfloat16"),
    "RL": ("sbuf", [128, RO * JW], "float32"),
}
for _i in range(8):
    SCRATCH["B%d" % _i] = ("psum", [128, 512], "float32")
SEMAPHORES = ["sV", "sS", "sP", "sG"] + ["ld%d" % i for i in range(6)] + ["st%d" % i for i in range(14)] \
    + [s + str(i) for s in ("arr", "ls", "ra", "na", "nl", "rn") for i in range(RO)]


CYC, GAT, SCA, WAKE, SLACK = 0.001, 1.5, 3.8, 0.15, 0.1
PLAN = {}
SEED = [8067, 0.3]
QW = {"V": 1.0, "S": 1.0, "P": 1.0, "G": 1.0, "Y": 1.0, "N": 1.0}
NEGV = V


def plan(ops):
    n = len(ops)
    pred = [dict() for _ in range(n)]
    succ = [[] for _ in range(n)]
    hist, last = {}, {}
    for i, (q, tag, reads, writes, occ, dur, _) in enumerate(ops):
        for w, lst in ((False, reads), (True, writes)):
            for _a, buf, m in lst:
                ps = buf in SCRATCH and SCRATCH[buf][0] == "psum"
                for em, ew, j in hist.get(buf, []):
                    same = ops[j][1] == tag
                    if j == i or (not (em & m and (w or ew)) and not ps) or (ps and same and q == "V" and not (em & m and (w or ew))):
                        continue
                    lat = 0.0 if same and (q == "P" or not ew) else WAKE
                    if pred[i].get(j, -1.0) < lat:
                        pred[i][j] = lat
        for w, lst in ((False, reads), (True, writes)):
            for _a, buf, m in lst:
                h = hist.setdefault(buf, [])
                ps = buf in SCRATCH and SCRATCH[buf][0] == "psum"
                if w and not ps:
                    h[:] = [e for e in h if e[0] & ~m or e[2] == i]
                h.append((m, w, i))
                if ps and len(h) > 150:
                    h[:] = h[-150:]
    for i in range(n):
        for j, lat in pred[i].items():
            succ[j].append((i, lat))
    pr = [0.0] * n
    for i in range(n - 1, -1, -1):
        pr[i] = ops[i][5] * QW[ops[i][0]] + max([lat + pr[k] for k, lat in succ[i]] + [0.0])
    if SEED[0]:
        pr = [float(x) for x in np.array(pr) + SEED[1] * np.random.default_rng(SEED[0]).random(n)]
    left = [len(p) for p in pred]
    est = [0.0] * n
    ready, free = {}, {}
    for i in range(n):
        free[ops[i][0]] = 0.0
        ready.setdefault(ops[i][0], [])
        if not left[i]:
            ready[ops[i][0]].append(i)
    out = []
    for _ in range(n):
        best = None
        for q in ready:
            if ready[q]:
                s0 = min(max(free[q], est[i]) for i in ready[q])
                k = max((i for i in ready[q] if max(free[q], est[i]) <= s0 + SLACK), key=lambda i: (pr[i], -i))
                s = max(free[q], est[k])
                if best is None or s < best[0]:
                    best = (s, q, k)
        s, q, k = best
        ready[q].remove(k)
        free[q] = s + ops[k][4]
        out.append(k)
        for i, lat in succ[k]:
            est[i] = max(est[i], s + ops[k][5] + lat)
            left[i] -= 1
            if not left[i]:
                ready[ops[i][0]].append(i)
    return out


def route(topo, src, dst):
    if topo.may_write(src, dst):
        return None
    c = [r for r in topo.cores_of(src) if r != src and topo.may_write(r, dst)]
    return sorted(c, key=lambda r: (topo.die(r) != topo.die(src), r))[0]


def emask(topo, src, dst):
    m = 0
    for e in topo.engines(src, dst)[:8]:
        m |= 1 << e
    return m


def relay_program(g, core, T, topo):
    for r in range(N):
        src = T.cores[r]
        for t in range(RO):
            dst = T.cores[(r + 1 + t % 3) % N]
            if route(topo, src, dst) == core:
                rid, pid = topo.addr(dst, core)
                m = emask(topo, core, dst)
                g.wait_ge(T.sem["rn%d" % t], 8)
                g.remote_dma(T.NN[:, t:t + 1], T.RN[:, t:t + 1], T.sem["na%d" % t], T.sem["nl%d" % t], pid, rid, m)
                g.wait_ge(T.sem["ra%d" % t], 8)
                g.remote_dma(T["C%d" % t][:, NP:CW], T.RL[:, t * JW:(t + 1) * JW], T.sem["arr%d" % t], T.sem["ls%d" % t], pid, rid, m)
    for r in range(N):
        for t in range(RO):
            if route(topo, T.cores[r], T.cores[(r + 1 + t % 3) % N]) == core:
                g.wait_ge(T.sem["nl%d" % t], 8)
                g.wait_ge(T.sem["ls%d" % t], 8)


def rank_program(g, core, T, topo):
    rank = T.rank_of(core)
    if rank is None:
        relay_program(g, core, T, topo)
        return
    eng = {"V": g.vector, "S": g.scalar, "P": g.tensor, "G": g, "Y": g.sync}
    cnt = {"V": 0, "S": 0, "P": 0, "G": 0}
    known = {q: {} for q in eng}
    hist = {}
    bits = {}
    serial = [0]

    def cols(lo, n, step):
        k = (lo, n, step)
        if k not in bits:
            m = 0
            for i in range(n):
                m |= 1 << (lo + i * step)
            bits[k] = m
        return bits[k]

    def a(buf, lo=0, n=None, step=1, p=None, p0=0):
        if n is None:
            n = T[buf].shape[1] - lo
        p = T[buf].shape[0] if p is None else p
        return (T[buf][p0:p0 + p, lo:lo + (n - 1) * step + 1:step] if step > 1 else T[buf][p0:p0 + p, lo:lo + n], buf, cols(lo, n, step))

    def ind(w, o):
        return (w[0].indirect(o[0]), w, o)

    def acc(x):
        return [x] if len(x) == 3 and isinstance(x[1], str) else [x[1], x[2]]

    def need(q, tag, reads, writes):
        want = {}
        for w, lst in ((False, reads), (True, writes)):
            for _, buf, m in lst:
                ps = buf[0] == "B" and buf[1:].isdigit()
                for (em, ew, eq, sem, val, snap) in hist.get(buf, []):
                    hit = em & m
                    if ps and eq != tag:
                        pass
                    elif not hit or not (w or ew):
                        continue
                    elif eq == tag and (not ew or (w and q == "P")):
                        continue
                    if known[q].get(sem, 0) >= val:
                        continue
                    if sem not in want or want[sem][0] < val:
                        want[sem] = (val, snap)
        for sem in list(want):
            val = want[sem][0]
            if any(o != sem and want[o][1].get(sem, 0) >= val for o in want):
                del want[sem]
        for sem in want:
            val, snap = want[sem]
            eng[q].wait_ge(T.sem[sem], val)
            for k, x in snap.items():
                if known[q].get(k, 0) < x:
                    known[q][k] = x
            known[q][sem] = max(known[q].get(sem, 0), val)

    def note(tag, reads, writes, sem, val, snap):
        for _, buf, m in writes:
            h = hist.setdefault(buf, [])
            h[:] = [e for e in h if e[0] & ~m] if not (buf[0] == "B" and buf[1:].isdigit()) else [e for e in h if e[2] != tag or e[0] & ~m]
            h.append((m, True, tag, sem, val, snap))
        for _, buf, m in reads:
            h = hist.setdefault(buf, [])
            h[:] = [e for e in h if e[1] or e[2] != tag or e[0] & ~m]
            h.append((m, False, tag, sem, val, snap))

    ops = []

    def run(q, fn, out, ins, cost):
        writes = acc(out)[:1] if isinstance(out, tuple) else out
        reads = acc(out)[1:] if isinstance(out, tuple) else []
        for x in ins:
            reads = reads + acc(x)

        def issue():
            need(q, q, reads, writes)
            cnt[q] += 1
            fn().then_inc(T.sem["s" + q], 1)
            snap = dict(known[q])
            snap["s" + q] = cnt[q]
            note(q, reads, writes, "s" + q, cnt[q], snap)
        ops.append((q, q, reads, writes, cost, cost, issue))

    def dma(q, out, in_, sem, reads, writes, dur=2.5):
        serial[0] += 1
        tag = "d%d" % serial[0]

        def issue():
            need(q, None, reads, writes)
            eng[q].dma_start(out, in_).then_inc(T.sem[sem], 16)
            note(tag, reads, writes, sem, 16, dict(known[q]))
        ops.append((q, tag, reads, writes, 0.05, dur, issue))

    def cost(out, ins, per):
        for x in ins:
            if isinstance(x[1], tuple):
                return 0.05 + GAT * CYC * 16 * bin(x[2][2]).count("1")
        if isinstance(out[1], tuple):
            return 0.05 + SCA * CYC * 16 * bin(out[2][2]).count("1")
        two = all(SCRATCH[x[1]][2] in ("bfloat16", "uint16") for x in [out] + ins)
        return CYC * max(64, bin(out[2]).count("1") * (per if per == 2 or not two else 0.5))

    def ap(x):
        return x[0]

    def copy(out, in_):
        run("V", lambda: g.vector.tensor_copy(ap(out), ap(in_)), out, [in_], cost(out, [in_], 1))

    def tt(out, x, y, op):
        ps = any(isinstance(z[1], str) and SCRATCH[z[1]][0] == "psum" for z in (x, y))
        run("V", lambda: g.vector.tensor_tensor(ap(out), ap(x), ap(y), op), out, [x, y], cost(out, [x, y], 1 if ps else 2))

    def ts(out, x, s1, op0, s2=None, op1=None):
        ins = [x] + [s for s in (s1, s2) if isinstance(s, tuple)]
        u1 = s1[0] if isinstance(s1, tuple) else s1
        if op1 is None:
            run("V", lambda: g.vector.tensor_scalar(ap(out), ap(x), u1, None, op0), out, ins, cost(out, [x], 1))
        else:
            run("V", lambda: g.vector.tensor_scalar(ap(out), ap(x), u1, s2, op0, op1), out, ins, cost(out, [x], 1))

    def scan(out, d0, d1, ini, op0, op1):
        run("V", lambda: g.vector.tensor_tensor_scan(ap(out), ap(d0), ap(d1), ini, op0, op1), out, [d0, d1], cost(out, [d0, d1], 1))

    def fill(out, c):
        run("V", lambda: g.vector.memset(ap(out), c), out, [], cost(out, [], 1))

    def act(out, x, func, bias=0.0, scale=1.0, accum=None):
        ins = [x] + ([bias] if isinstance(bias, tuple) else [])
        b = bias[0] if isinstance(bias, tuple) else bias
        if accum is None:
            if isinstance(out[1], tuple):
                run("S", lambda: g.scalar.activation(ap(out), ap(x), func), out, ins, cost(out, [x], 1))
                return
            c = cost(out, [x], 2) if isinstance(x[1], tuple) else CYC * max(64, bin(out[2]).count("1"))
            run("S", lambda: g.scalar.activation(ap(out), ap(x), func, bias=b, scale=scale), out, ins, c)
        else:
            run("S", lambda: g.scalar.activation(ap(out), ap(x), func, bias=b, scale=scale, accum_out=ap(accum)), [out, accum], ins,
                CYC * bin(out[2]).count("1"))

    def mm(out, l, r, start, stop):
        c = CYC * max(min(64, bin(l[2]).count("1")), bin(r[2]).count("1")) * (4 if SCRATCH[l[1]][2] == "float32" else 1)
        run("P", lambda: g.tensor.matmul(ap(out), ap(l), ap(r), start, stop), out, [l, r], c)

    def iota(out, pat, base, cm):
        run("G", lambda: g.iota(ap(out), pat, base, cm, allow_small_or_imprecise_dtypes=True), out, [], 0.13 + 2 * CYC * bin(out[2]).count("1"))

    def sel(out, x, pat, op, fl, base, cm):
        run("G", lambda: g.affine_select(ap(out), ap(x), pat, op, fl, base, cm), out, [x], 0.17 + 2 * CYC * bin(out[2]).count("1"))

    def send(t, src, land, relay, arr, ra, ls, lat):
        dst = T.cores[(rank + 1 + t % 3) % N]
        first = route(topo, core, dst)
        to = dst if first is None else first
        net = ("", "net" + arr, 1)

        def issue():
            need("G", None, [src], [])
            rid, pid = topo.addr(to, core)
            g.remote_dma(land[0] if first is None else relay, src[0], T.sem[(arr if first is None else ra) + str(t)], T.sem[ls + str(t)],
                         pid, rid, emask(topo, core, to))
            note("r%s%d" % (ls, t), [src], [], ls + str(t), 8, dict(known["G"]))
        ops.append(("G", "r%s%d" % (ls, t), [src], [net], 0.3, 2.0, issue))
        ops.append(("N", "q%s%d" % (arr, t), [net], [land], 0.0, lat * (1 if first is None else 2),
                    lambda: note("q%s%d" % (arr, t), [], [land], arr + str(t), 8, {})))

    dma("Y", T.FR[:], T.fr[:], "ld0", [], [a("FR")], 2.2)
    dma("Y", T.CI[:], T.cl[:], "ld2", [], [a("CI")], 4.0)
    dma("Y", T.W[:, XB:XB + V], T.xv[:], "ld3", [], [a("W", XB, V)], 6.0)
    dma("Y", T.TI[:], T.th[:], "ld1", [], [a("TI")], 6.0)
    fill(a("VM", 0, 16), 200.0)
    act(a("W", SB, 16), a("VM", 0, 16), F_.Silu)

    fill(a("ONE"), 1.0)
    fill(a("FRB"), 8.0)
    sel(a("PM"), a("ONE", 0, 416, p=16), [[0, 26], [1, 16]], A_.is_equal, 0.0, 0, -1)
    sel(a("QM0"), a("ONE", 0, 128, p=8), [[1, 128]], A_.is_ge, 0.0, 0, -16)
    sel(a("QM"), a("QM0"), [[-1, 128]], A_.is_ge, 0.0, 15, 16)
    fill(a("SEGM"), 1.0)
    fill(a("SEGM", 0, 64, 16), 0.0)
    mm(a("B1", 0, 416), a("PM", 0, 128), a("PM", 0, 416), True, True)
    mm(a("B2", 0, NP - 416), a("PM", 0, 128), a("PM", 0, NP - 416), True, True)
    mm(a("B3", 0, 128), a("QM"), a("QM"), True, True)
    copy(a("DM", 0, 416), a("B1", 0, 416))
    act(a("DM", 416, NP - 416), a("B2", 0, NP - 416), F_.Identity)
    copy(a("BO"), a("B3", 0, 128))
    for s0, p0, n in SEG:
        copy(a("FRB", p0, n), a("FR", s0, n))
    mm(a("B4", 0, 512), a("QM"), a("FRB", 0, 512), True, True)
    mm(a("B5", 0, NP - 512), a("QM"), a("FRB", 512, NP - 512), True, True)
    tt(a("FW", 0, 512), a("B4", 0, 512), a("DM", 0, 512), A_.mult)
    tt(a("FW", 512, NP - 512), a("B5", 0, NP - 512), a("DM", 512, NP - 512), A_.mult)
    scan(a("FWS"), a("SEGM", 0, NP), a("FW"), 0.0, A_.mult, A_.add)
    copy(a("T2"), a("FWS", 15, Q, 16))
    sel(a("TS"), a("BO"), [[1, 128]], A_.is_ge, 0.0, -1, -1)
    iota(a("CL0"), [[0, 8], [1, 16]], 0, 0)
    sel(a("CL"), a("CL0"), [[0, 128]], A_.is_gt, 1.0, 0, 1)
    iota(a("CR0", 0, Q), [[-16, Q]], -2 * K, 0)
    iota(a("CR0", Q, Q), [[-16, Q]], -K, 0)
    sel(a("CR"), a("CR0"), [[0, 2 * Q]], A_.is_equal, -1.0, 0, 1)

    def order(t):
        for b, s in ((0, START[AS * t % K]), (Q, START[FS * t % K])):
            u = "U%d" % t
            n = Q - s
            sel(a("UT", b + s, n, p=2 * Q), a("ONE", 0, n, p=2 * Q), [[1, n]], A_.is_gt, 0.0, b + s, -1)
            sel(a(u, b + s, n), a("UT", b + s, n), [[0, n]], A_.is_ge, 0.0, -(b + s), 1)
            if s:
                sel(a(u, b, s), a("ONE", 0, s, p=2 * Q), [[0, s]], A_.is_ge, 0.0, b + Q - 1, -1)
                sel(a("UT", b, s), a(u, b, s), [[0, s]], A_.is_ge, 0.0, -(b + s), 1)
                sel(a(u, b, s), a("UT", b, s), [[-1, s]], A_.is_ge, 1.0, -b, 1)
                if b:
                    sel(a("UT", b, s), a(u, b, s), [[0, s]], A_.is_ge, 0.0, -b, 1)
                    sel(a(u, b, s), a("UT", b, s), [[0, s]], A_.is_ge, 0.0, -b, 1)

    order(0)
    mm(a("B6", 0, Q), a("CL"), a("CR", 0, Q), True, True)
    ts(a("PD"), a("B6", 0, Q), -1.0, A_.mult)
    ts(a("J0"), a("PD"), -2.0 * K, A_.add)
    ts(a("JD"), a("J0", 0, 8), float(JW - 512), A_.add)
    iota(a("LN", 0, LA), [[0, LA]], 2 * V + int(OFF), 0)
    iota(a("LN", FB0, LF), [[0, LF]], 2 * V + int(OFF), 0)

    def lists(t):
        ts(a("FL", 0, Q), a("T2"), 0.0, A_.is_le)
        ts(a("GE"), a("T2"), 0.0, A_.is_gt)
        ts(a("FL", 2 * Q, Q), a("T2"), 3.5, A_.is_ge)
        tt(a("FL", Q, Q), a("GE"), a("FL", 2 * Q, Q), A_.subtract)
        mm(a("B7", 0, 128, p=2 * Q), a("FL", 0, 2 * Q), a("BO"), True, True)
        act(a("O1"), a("B7", 0, 128, p=2 * Q), F_.Identity)
        mm(a("B6", 0, 2 * Q), a("TS"), a("FL", 0, 2 * Q), True, False)
        mm(a("B6", 0, 2 * Q), a("CL"), a("CR"), False, False)
        mm(a("B6", 0, 2 * Q), a("O1"), a("U%d" % t), False, True)
        ts(a("F1"), a("T2"), 0.0, A_.max, 1.0, A_.add)
        tt(a("MM"), a("B6", 0, 2 * Q), a("FL", 0, 2 * Q), A_.mult)
        tt(a("PS", 0, Q), a("MM", 0, Q), a("MM", Q, Q), A_.add)
        tt(a("PS", Q, Q), a("PS", 0, Q), a("PD"), A_.add)
        copy(a("PL", 0, Q), a("PS", Q, Q))
        act(ind(a("LN"), a("PL", 0, Q)), a("C%d" % t, 0, NP), F_.Silu)
        ts(a("OA"), a("LN", 0, LA), 0.25 - OFF, A_.add)
        ts(a("OF"), a("LN", FB0, LF), 0.25 - OFF, A_.add)
        mm(a("B5", 0, 128, p=Q), a("FL", 2 * Q, Q), a("BO"), True, True)
        act(a("O2"), a("B5", 0, 128, p=Q), F_.Identity)
        mm(a("B5", 128, Q), a("TS"), a("FL", 2 * Q, Q), True, False)
        mm(a("B5", 128, Q), a("NI4"), a("FL", 2 * Q, Q), False, False)
        mm(a("B5", 128, Q), a("O2"), a("U0", 0, Q, p=Q), False, True)

    def gather(q, c, out, off):
        w = ind(a("W", XB, WW - XB), a(off, CH * c, CH))
        if q == "V":
            copy(a(out, 16 * CH * c, 16 * CH), w)
        else:
            act(a(out, 16 * CH * c, 16 * CH), w, F_.Identity)

    def negate(lo, n, q):
        if q == "V":
            ts(a("W", XB + V + lo, n), a("W", XB + lo, n), -1.0, A_.mult, 63.0, A_.add)
        else:
            act(a("W", XB + V + lo, n), a("W", XB + lo, n), F_.Identity, 63.0, -1.0)

    for s0, p0, n in SEG:
        fill(a("C0", p0 + n, -(-n // 16) * 16 - n), OFF)
        ts(a("C0", p0, n), a("CI", s0, n), OFF, A_.add)
    sel(a("ID"), a("ONE", 0, 128), [[-1, 128]], A_.is_equal, 0.0, 0, 1)
    ts(a("NI4"), a("ID"), -4096.0, A_.mult)
    lists(0)
    negate(0, V, "S")
    fill(a("W", 0, XB), 0.0)
    fill(a("RST"), 64.0)
    fill(a("RST", 0, 64, 16), 8192.0)
    copy(a("TH"), a("TI"))
    copy(a("TT"), a("TI"))
    pads = 0
    for s0, p0, n in SEG:
        fill(a("DC", p0 // 16, -(-n // 16)), 4096.0 - 513.0 - pads)
        pads += -(-n // 16) * 16 - n
    ts(a("PS", 0, Q), a("T2"), 6.0, A_.is_ge, 4096.0, A_.mult)
    tt(a("DC"), a("DC"), a("PS", 0, Q), A_.add)
    fill(a("YW"), 1.0)
    fill(a("FBB"), 0.0)
    fill(a("JB"), 0.0)
    fill(a("O32"), 1.0 / 32)
    copy(a("BOF"), a("BO"))
    sel(a("SH"), a("BOF"), [[-1, 128]], A_.is_equal, 0.0, -1, 1)
    tt(a("DF"), a("ID"), a("SH"), A_.subtract)
    ts(a("D1024"), a("DF"), -1024.0, A_.mult)
    ts(a("D8"), a("DF"), -8.0, A_.mult)
    ts(a("I4"), a("ID"), 4096.0, A_.mult)
    ts(a("I16"), a("BO", 0, 8, 16), 16.0, A_.mult)
    ts(a("NIN"), a("BO", 0, 8, 16), -1.0, A_.mult)
    ts(a("KV"), a("DM", 15, 1), float(XB - V // 2 - 4096 - OFF), A_.mult)
    iota(a("KC0"), [[0, 16], [-16384, 16]], 262144, 0)
    iota(a("KC1"), [[0, 16], [-1, 16]], 15, 0)
    iota(a("KW"), [[0, 8], [1024, 16]], -16384, 0)
    tt(a("WC"), a("BO"), a("KW"), A_.mult)
    iota(a("LQI", 52, 16), [[16, 16]], 15, 0)
    copy(a("L15"), a("LQI", 52, 16))
    iota(a("LQI", 0, 52), [[1, 52]], 0, 0)
    copy(a("LQ"), a("LQI", 0, 52))
    sel(a("LT"), a("ONE", 0, 256, p=16), [[0, 16], [-1, 16]], A_.is_ge, 0.0, -1, 1)
    mm(a("B4", 0, 256), a("PM", 0, 128), a("LT"), True, True)
    act(a("TRI"), a("B4", 0, 256), F_.Identity)

    for t in range(RO):
        C = "C%d" % t
        gather("S", 0, "S", "OA")
        gather("V", 1, "S", "OA")
        gather("S", 2, "S", "OA")
        gather("S", 3, "S", "OA")
        ts(a("LX"), a("OA"), OFF, A_.add)
        tt(a("DEO"), a("LX", 1, 128, 2), a("LX", 0, 128, 2), A_.subtract)
        tt(a("DD"), a("B5", 128, Q), a("DC"), A_.add)
        ts(a("EN", Q, Q), a("DD"), 513.0 + NP, A_.add)
        tt(a("EN", 0, Q), a("J0"), a("EN", Q, Q), A_.subtract)
        act(a("SG"), a("LN", 0, LA), F_.Sign, 0.5 - V - OFF)
        for h in range(2):
            mm(a("B2", 128 * h, 128), a("DF"), a("LX", h, 128, 2), True, False)
            mm(a("B2", 128 * h, 128), a("D1024"), a("SG", h, 128, 2), False, True)
            mm(a("B2", 256 + 128 * h, 128), a("D8"), a("SG", h, 128, 2), True, True)
        act(a("DLV"), a("B2", 0, 256), F_.Identity, a("KV"))
        act(a("DLS"), a("B2", 256, 256), F_.Identity)
        mm(a("B0", 0, 256), a("ONE", 0, 128, p=1), a("KC0"), True, False)
        for c in range(NF):
            gather("S", c, "S2", "OF")
        for c in range(NA):
            lo = 16 * CH * c
            scan(a("M", lo, 16 * CH), a("SEGM"), a("S", lo, 16 * CH), 0.0, A_.mult, A_.max)
            ts(a("FA", CH * c, CH), a("M", lo + 15, CH, 16), a("TT"), A_.is_lt)
            ts(a("VV", CH * c, CH), a("FA", CH * c, CH), 2048.0, A_.mult, -1024.0, A_.add)
            tt(a("S", lo, CH, 16), a("VV", CH * c, CH), a("M", lo, CH, 16), A_.min)
            scan(a("Z", lo, 16 * CH), a("RST"), a("S", lo, 16 * CH), 0.0, A_.add, A_.min)
            if c == NA - 1:
                mm(a("B4", 0, LA), a("BO"), a("FA"), True, True)
            for h in range(2):
                mm(a("B0", 128 * h, 128, p=32, p0=32 * c), a("FA", CH * c + h, 32, 2), a("WC"), False, False)
            for h in range(2):
                for k in range(16):
                    mm(a("B0", 128 * h + k, 8, 16, p=32, p0=32 * c), a("Z", lo + 16 * h + k, 32, 32), a("I16"), False, False)
        mm(a("B0", 0, 256), a("ONE", 0, 128, p=1), a("KC1"), False, True)
        ts(a("VI"), a("B4", 0, LA), 3.5, A_.is_gt)
        act(a("YW", 0, LA), a("B4", 0, LA), F_.Relu, -25.0, 8.0)
        act(a("SGJ"), a("B4", 0, LA), F_.Sign, -3.5, 1.0, a("SGA"))
        tt(a("BT"), a("VI", 0, 128, 2), a("VI", 1, 128, 2), A_.mult)
        scan(a("INC"), a("ONE", 0, 128), a("BT"), -513.0, A_.mult, A_.add)
        tt(a("IB"), a("INC"), a("BT"), A_.mult)
        tt(a("IBD"), a("IB"), a("DM", 0, 128), A_.mult)
        scan(a("IS"), a("SEGM", 0, 128), a("IBD"), 0.0, A_.mult, A_.add)
        tt(a("JL"), a("IS", 15, 8, 16), a("JD"), A_.min)
        ts(a("JLU"), a("JL"), 512.0, A_.add)
        send(t, a("INC", 127, 1), a("NN", t, 1), T.RN[:, t:t + 1], "na", "rn", "nl", 2.0)
        scan(a("R"), a("SEGM", 0, 256), a("B0", 0, 256), 0.0, A_.mult, A_.max)
        scan(a("VT"), a("SEGM", 0, 256), a("B0", 0, 256), 0.0, A_.mult, A_.max)
        tt(a("EQ"), ind(a("R"), a("L15")), a("VT"), A_.is_equal)
        for h in range(2):
            mm(a("B3", 128 * h, 128), a("EQ", 128 * h, 128), a("ID"), True, True)
        scan(a("M2", 0, 1024), a("SEGM"), a("S2", 0, 1024), 0.0, A_.mult, A_.max)
        tt(a("HV"), a("B3", 0, 256), a("DLV"), A_.mult)
        tt(a("HS"), a("B3", 0, 256), a("DLS"), A_.mult)
        for h in range(2):
            mm(a("B1", h, 128, 2), a("BOF"), a("HV", 128 * h, 128), True, False)
            mm(a("B1", h, 128, 2), a("I4"), a("VI", h, 128, 2), False, True)
        for h in range(2):
            mm(a("B7", h, 128, 2), a("BO"), a("HS", 128 * h, 128), True, True)
        scan(a("M2", 1024, 1024), a("SEGM"), a("S2", 1024, 1024), 0.0, A_.mult, A_.max)
        for k in range(16):
            mm(a("B2", k, 8, 16), a("S", 16 + k, 128, 32) if k else a("M", 16, 128, 32), a("BO", 0, 8, 16), True, False)
            mm(a("B2", k, 8, 16), a("S", k, 128, 32) if k else a("M", 0, 128, 32), a("NIN"), False, True)
        tt(a("VM"), a("B1", 0, 256), a("DM", 0, 256), A_.mult)
        tt(a("VT"), a("B1", 0, 256), a("TRI"), A_.mult)
        scan(a("CS"), a("SEGM", 0, 256), a("VM"), 0.0, A_.mult, A_.add)
        tt(a("FSG"), a("B7", 0, 256), a("FA"), A_.mult)
        tt(a("EE"), ind(a("CS"), a("L15")), a("VT"), A_.is_equal)
        copy(a("GL"), a("CS", 15, 16, 16))
        scan(a("ES"), a("SEGM", 0, 256), a("EE"), 0.0, A_.mult, A_.add)
        ts(a("W1", 0, 16), a("ES", 15, 16, 16), -8192.0, A_.mult)
        tt(a("W1", 16, 16), a("W1", 0, 16), a("CS", 15, 16, 16), A_.add)
        tt(a("W1", 32, 16), a("W1", 16, 16), a("J0", 0, 16), A_.max)
        copy(a("SL", 0, 16, 2), a("W1", 32, 16))
        ts(a("GT"), a("B2", 0, 128), 0.0, A_.is_gt)
        mm(a("B3", 256, 128), a("GT"), a("ID"), True, True)
        tt(a("XN"), ind(a("W", 0, XB + V), a("GL")), a("FSG"), A_.add)
        tt(a("PJ"), a("B3", 256, 128), a("DEO"), A_.mult)
        tt(ind(a("JB"), a("JLU")), a("PJ"), a("LX", 0, 128, 2), A_.add)
        send(t, a("JB", 0, JW), a(C, NP, JW), T.RL[:, t * JW:(t + 1) * JW], "arr", "ra", "ls", 2.2)
        ts(a("XC"), a("XN"), 0.0, A_.max, 63.0, A_.min)
        for b in range(15, -1, -1):
            copy(ind(a("W", 0, XB + V), a("SL", 2 * b, 1)), a("XC", 16 * b, 16))
        if t < RO - 1:
            iota(a("LN", 0, LA), [[0, LA]], 2 * V + int(OFF), 0)
            iota(a("LN", FB0, LF), [[0, LF]], 2 * V + int(OFF), 0)
            order(t + 1)
            if NEGV:
                negate(0, NEGV, "V")
            if NEGV < V:
                negate(NEGV, V - NEGV, "S")
        else:
            dma("Y", T.yx[:], T.W[:, XB:XB + V], "st0", [a("W", XB, V)], [], 4.5)
        scan(a("M2", 2048, 1024), a("SEGM"), a("S2", 2048, 1024), 0.0, A_.mult, A_.max)
        ts(a("FA2"), a("M2", 15, LF, 16), a("TT"), A_.is_lt)
        mm(a("B6", 0, LF), a("BO"), a("FA2"), True, True)
        act(a("YW", FB0, LF), a("B6", 0, LF), F_.Relu, -25.0, 8.0)
        if t < RO - 1:
            mm(a("B7", 256, 1), a("O32"), a("SGA"), True, True)
            copy(a("AI", 0, 1), a("B7", 256, 1))
            ts(a("AI", 1, 1), a("AI", 0, 1), 3, A_.bitwise_and)
            tt(a("TT"), a("TH"), a("AI", 1, 1), A_.add)
        tt(a("FW"), ind(a("YW"), a("PL", 0, Q)), a("DM"), A_.mult)
        ts(a("EN", 2 * Q, Q), a("DD"), a("NN", t, 1), A_.is_ge)
        tt(a("IXF", 0, Q), a("EN", 0, Q), a("EN", 2 * Q, Q), A_.mult)
        tt(a("IXF", Q, Q), a("IXF", 0, Q), a("EN", Q, Q), A_.add)
        copy(a("IX", 0, Q), a("IXF", Q, Q))
        act(a("C%d" % (t + 1), 0, NP), ind(a(C), a("IX", 0, Q)), F_.Identity, -OFF if t == RO - 1 else 0.0)
        scan(a("FWS"), a("SEGM", 0, NP), a("FW"), 0.0, A_.mult, A_.add)
        tt(a("T1"), a("F1"), a("FWS", 15, Q, 16), A_.subtract)
        tt(a("T2"), a("T1"), a("EN", 2 * Q, Q), A_.mult)
        if t < RO - 1:
            lists(t + 1)
    for i, (s0, p0, n) in enumerate(SEG):
        dma("Y" if i % 2 else "S", T.yc[:, s0:s0 + n], T.C3[:, p0:p0 + n], "st%d" % (1 + i), [a("C3", p0, n)], [])
    ts(a("FBB", 0, Q), a("T2"), 0.0, A_.max)
    tt(a("FW"), ind(a("FBB"), a("LQ", 0, Q)), a("DM"), A_.mult)
    mm(a("B4", 0, 512, p=8), a("BO", 0, 8, 16), a("FW", 0, 512), True, True)
    mm(a("B6", 0, NP - 512, p=8), a("BO", 0, 8, 16), a("FW", 512, NP - 512), True, True)
    act(a("YF8", 0, 512), a("B4", 0, 512, p=8), F_.Identity)
    copy(a("YF8", 512, NP - 512), a("B6", 0, NP - 512, p=8))
    for i, (s0, p0, n) in enumerate(SEG):
        dma("Y" if i % 2 else "S", T.yf[:, s0:s0 + n], T.YF8[:, p0:p0 + n], "st%d" % (6 + i), [a("YF8", p0, n)], [])
    if "order" not in PLAN:
        PLAN["order"] = plan(ops)
    for i in PLAN["order"]:
        ops[i][6]()
    for q in cnt:
        g.wait_ge(T.sem["s" + q], cnt[q])
    for i in range(4):
        g.wait_ge(T.sem["ld%d" % i], 16)
    for i in range(11):
        g.wait_ge(T.sem["st%d" % i], 16)
    for t in range(RO):
        for s in ("ls", "arr", "nl", "na"):
            g.wait_ge(T.sem[s + str(t)], 8)
